import numpy as np
import ml_dtypes


def mxq(x, axis, fmt="e4m3"):
    dtype, down = {"e4m3": (ml_dtypes.float8_e4m3fn, 7), "e5m2": (ml_dtypes.float8_e5m2, 14)}[fmt]
    v = np.moveaxis(np.asarray(x, np.float32).astype(ml_dtypes.bfloat16).astype(np.float64), axis, -1)
    blocks = v.reshape(v.shape[:-1] + (-1, 32))
    amax = np.abs(blocks).max(-1, keepdims=True)
    byte = np.maximum(np.where(amax > 0, np.frexp(amax)[1] - 1 + 127, 0) - down, 1)
    scale = np.exp2(byte - 127.0)
    codes = (blocks / scale).astype(np.float32).astype(dtype).astype(np.float64)
    return np.moveaxis((codes * scale).reshape(v.shape), -1, axis)


WIDE = False


def mx_kscale(k):
    if not WIDE:
        return np.ones(k)
    levels = np.array([10, -10, 5, -5, 0])
    if k % 512:
        return np.exp2(np.random.permutation(np.resize(levels, k // 32))).repeat(32)
    a = np.empty((k // 512, 16))
    for p in range(k // 512):
        a[p, :8] = np.random.permutation(np.resize(levels, 8))
        for g in range(8):
            far = levels[np.abs(levels - a[p, g]) >= 10]
            a[p, g + 8] = far[np.random.randint(len(far))]
    return np.exp2(a.ravel()).repeat(32)


def f64(x):
    return np.asarray(x).astype(np.float64)


def striped(idx):
    return np.tile(idx.reshape(-1, 16).T, (8, 1)).astype(np.uint16)


def unstriped(offs):
    return offs[:16].T.reshape(-1).astype(np.int64)


def sigmoid(v):
    return 1.0 / (1.0 + np.exp(-np.maximum(v, -700.0)))


K, T, S, N, U = 512, 2048, 1024, 256, 1024


def setup_inputs():
    n = np.random.standard_normal
    s = mx_kscale(K)[:, None]
    return {
        "xT": (n((K, T)) * s).astype(np.float32),
        "w1": (n((K, N)) / np.sqrt(K) / s).astype(np.float32),
        "w2": (n((K, N)) / np.sqrt(K) / s).astype(np.float32),
        "w3": (n((K, N)) / np.sqrt(K) / s).astype(np.float32),
        "offs": striped(np.random.permutation(T)[:S]),
        "src": striped(np.random.permutation(S)[(S * np.random.uniform(0, 1, U) ** 4).astype(np.int64)]),
        "dst": striped(np.random.permutation(S)),
    }


def reference(xT, w1, w2, w3, offs, src, dst):
    xq = mxq(f64(xT)[:, unstriped(offs)], 0, "e4m3")
    y = mxq(f64(w1), 0, "e4m3").T @ xq
    e = mxq(f64(w2), 0, "e4m3").T @ xq
    h = mxq(f64(w3), 0, "e4m3").T @ xq
    return (sigmoid(y[:, unstriped(dst)] + e[:, unstriped(src)])) * h[:, unstriped(src)]

@@ -1,0 +1,167 @@
+from contextlib import ExitStack
+
+import concourse.mybir as mybir
+
+K, T, S, N, U = 512, 2048, 1024, 256, 1024
+FLOPS = 3 * 2 * K * N * S
+
+F32 = mybir.dt.float32
+BF16 = mybir.dt.bfloat16
+U32 = mybir.dt.uint32
+U16 = mybir.dt.uint16
+U8 = mybir.dt.uint8
+FP8X4 = mybir.dt.float8_e4m3fn_x4
+ADD = mybir.AluOpType.add
+MULT = mybir.AluOpType.mult
+SIGMOID = mybir.ActivationFunctionType.Sigmoid
+
+P = 128
+PACK = 4
+BANK = 512
+CHUNKS = ((1024, 512, 512), (512, 512, 512, 256, 256))
+PIECES = ((0, 256), (256, 512), (512, 768), (768, 1024))
+HALVES = ((0, 512), (512, 1024))
+LAST = ((0, 512), (512, 768), (768, 1024))
+
+
+def entries(offsets, lo, hi):
+    return offsets[:, lo // 16 : hi // 16]
+
+
+def tile_picked_edgeatt_sigmoid_e_kernel(tc, xT, w1, w2, w3, offs, src, dst, out):
+    nc = tc.nc
+    with ExitStack() as ctx:
+        keep = ctx.enter_context(tc.tile_pool(name="keep", bufs=1))
+        psum = ctx.enter_context(tc.psum_pool(name="psum", bufs=8))
+
+        x_rows = xT.rearrange("(p j) t -> p j t", j=PACK)
+        offs_sb = keep.tile([P, S // 16], U16, name="offs_sb")
+        src_sb = keep.tile([P, U // 16], U16, name="src_sb")
+        dst_sb = keep.tile([P, U // 16], U16, name="dst_sb")
+
+        raw = {}
+        for u in range(2):
+            lo = 0
+            for c, width in enumerate(CHUNKS[u]):
+                raw[u, c] = keep.tile([P, 2, width], F32, name="raw%d_%d" % (u, c))
+                nc.sync.dma_start(out=raw[u, c][:], in_=x_rows[:, 2 * u : 2 * u + 2, lo : lo + width])
+                lo = lo + width
+                if (u, c) == (0, 1):
+                    nc.sync.dma_start(offs_sb[:], offs)
+        w_raw = []
+        for i, w in enumerate((w1, w2, w3)):
+            w_raw.append(keep.tile([P, PACK, N], F32, name="w_raw%d" % i))
+            nc.sync.dma_start(out=w_raw[i][:], in_=w.rearrange("(p j) n -> p j n", j=PACK))
+        nc.sync.dma_start(dst_sb[:], dst)
+        nc.sync.dma_start(src_sb[:], src)
+
+        pairs = [keep.tile([P, T], U32, name="pairs%d" % u, align_bytes=64) for u in range(2)]
+        picked = keep.tile([P, S, 2], U32, name="picked", align_bytes=64)
+
+        def cast(u, c, on_vector):
+            lo = sum(CHUNKS[u][:c])
+            width = CHUNKS[u][c]
+            target = pairs[u][:, lo : lo + width].bitcast(BF16).rearrange("p (t e) -> p t e", e=2)
+            source = raw[u, c][:].rearrange("p e t -> p t e")
+            if on_vector:
+                nc.vector.tensor_copy(out=target, in_=source)
+            else:
+                nc.scalar.copy(out=target, in_=source)
+
+        def pick(u):
+            nc.vector.tensor_copy(out=picked[:, :, u], in_=pairs[u][:].indirect(offs_sb[:]))
+
+        w_bf = [keep.tile([P, N, PACK], BF16, name="w_bf%d" % i, tag="staged%d" % i, align_bytes=64) for i in range(3)]
+        x_codes = keep.tile([P, S], U32, name="x_codes", tag="staged0", align_bytes=64)
+        x_scales = keep.tile([P, S], U8, name="x_scales", align_bytes=64)
+
+        def quantise_x(i):
+            lo, hi = PIECES[i]
+            nc.vector.quantize_mx(
+                out=x_codes[:, lo:hi].bitcast(FP8X4),
+                scales=x_scales[:, lo:hi],
+                in_=picked[:, lo:hi, :].rearrange("p n u -> p (n u)").bitcast(BF16),
+            )
+
+        w_codes = [keep.tile([P, N], U32, name="w_codes%d" % i, align_bytes=64) for i in range(3)]
+        w_scales = [keep.tile([P, N], U8, name="w_scales%d" % i, align_bytes=64) for i in range(3)]
+
+        def group_w(i):
+            nc.scalar.copy(out=w_bf[i][:], in_=w_raw[i][:].rearrange("p j n -> p n j"))
+
+        def quantise_w(i):
+            nc.vector.quantize_mx(
+                out=w_codes[i][:].bitcast(FP8X4),
+                scales=w_scales[i][:],
+                in_=w_bf[i][:].rearrange("p n j -> p (n j)"),
+            )
+
+        res = {}
+        for i in range(3):
+            for b in range(2):
+                res[i, b] = keep.tile([P, S], F32, name="res%d_%d" % (i, b))
+
+        def product(i, b, lo, hi, on_vector=False):
+            acc = psum.tile([P, BANK], F32, name="acc")
+            cols = slice(b * P, (b + 1) * P)
+            nc.tensor.matmul_mx(
+                out=acc[:, : hi - lo],
+                lhsT=w_codes[i][:, cols].bitcast(FP8X4),
+                lhsT_scale=w_scales[i][:, cols],
+                rhs=x_codes[:, lo:hi].bitcast(FP8X4),
+                rhs_scale=x_scales[:, lo:hi],
+                start=True,
+                stop=True,
+            )
+            if on_vector:
+                nc.vector.tensor_copy(out=res[i, b][:, lo:hi], in_=acc[:, : hi - lo])
+            else:
+                nc.scalar.copy(out=res[i, b][:, lo:hi], in_=acc[:, : hi - lo])
+
+        for c in range(len(CHUNKS[0])):
+            cast(0, c, True)
+        for c in range(len(CHUNKS[1]) - 2):
+            cast(1, c, False)
+        pick(0)
+        cast(1, len(CHUNKS[1]) - 2, True)
+        cast(1, len(CHUNKS[1]) - 1, True)
+        pick(1)
+        group_w(0)
+        group_w(1)
+        group_w(2)
+        quantise_w(0)
+        for i in range(len(PIECES)):
+            quantise_x(i)
+        quantise_w(1)
+        for i in range(len(PIECES)):
+            product(0, 0, *PIECES[i])
+        quantise_w(2)
+
+        y_dst = [keep.tile([P, U], F32, name="y_dst%d" % b) for b in range(2)]
+        logit = [keep.tile([P, U], F32, name="logit%d" % b) for b in range(2)]
+        gate = [keep.tile([P, U], F32, name="gate%d" % b) for b in range(2)]
+        result = [keep.tile([P, U], F32, name="result%d" % b) for b in range(2)]
+
+        def fetch_y(b):
+            for lo, hi in HALVES:
+                nc.vector.tensor_copy(out=y_dst[b][:, lo:hi], in_=res[0, b][:].indirect(entries(dst_sb, lo, hi)))
+
+        def add_e(b):
+            for lo, hi in HALVES:
+                nc.vector.tensor_tensor(logit[b][:, lo:hi], res[1, b][:].indirect(entries(src_sb, lo, hi)), y_dst[b][:, lo:hi], ADD)
+            nc.scalar.activation(gate[b][:], logit[b][:], SIGMOID)
+
+        def times_h(b, cuts):
+            for lo, hi in cuts:
+                nc.vector.tensor_tensor(result[b][:, lo:hi], res[2, b][:].indirect(entries(src_sb, lo, hi)), gate[b][:, lo:hi], MULT)
+                nc.sync.dma_start(out=out[b * P : (b + 1) * P, lo:hi], in_=result[b][:, lo:hi])
+
+        for i, b in ((1, 0), (0, 1), (1, 1), (2, 0), (2, 1)):
+            for lo, hi in HALVES:
+                product(i, b, lo, hi)
+        fetch_y(0)
+        add_e(0)
+        fetch_y(1)
+        add_e(1)
+        times_h(0, HALVES)
+        times_h(1, LAST)

@@ -7,6 +7,7 @@ FLOPS = 3 * 2 * K * N * S
 
 F32 = mybir.dt.float32
 BF16 = mybir.dt.bfloat16
+I32 = mybir.dt.int32
 U32 = mybir.dt.uint32
 U16 = mybir.dt.uint16
 U8 = mybir.dt.uint8
@@ -19,9 +20,10 @@ P = 128
 PACK = 4
 BANK = 512
 CHUNKS = ((1024, 512, 512), (512, 512, 512, 256, 256))
-PIECES = ((0, 256), (256, 512), (512, 768), (768, 1024))
+PIECE = 256
+PIECES = S // PIECE
 HALVES = ((0, 512), (512, 1024))
-LAST = ((0, 512), (512, 768), (768, 1024))
+LAST = ((0, 512), (512, 896), (896, 1024))
 
 
 def entries(offsets, lo, hi):
@@ -32,7 +34,7 @@ def tile_picked_edgeatt_sigmoid_e_kernel(tc, xT, w1, w2, w3, offs, src, dst, out
     nc = tc.nc
     with ExitStack() as ctx:
         keep = ctx.enter_context(tc.tile_pool(name="keep", bufs=1))
-        psum = ctx.enter_context(tc.psum_pool(name="psum", bufs=8))
+        psum = ctx.enter_context(tc.psum_pool(name="psum", bufs=1))
 
         x_rows = xT.rearrange("(p j) t -> p j t", j=PACK)
         offs_sb = keep.tile([P, S // 16], U16, name="offs_sb")
@@ -56,7 +58,8 @@ def tile_picked_edgeatt_sigmoid_e_kernel(tc, xT, w1, w2, w3, offs, src, dst, out
         nc.sync.dma_start(src_sb[:], src)
 
         pairs = [keep.tile([P, T], U32, name="pairs%d" % u, align_bytes=64) for u in range(2)]
-        picked = keep.tile([P, S, 2], U32, name="picked", align_bytes=64)
+        picked = [keep.tile([P, 2, PIECE], U32, name="picked%d" % i, align_bytes=64) for i in range(PIECES)]
+        woven = [keep.tile([P, PIECE, 2], U32, name="woven%d" % i, tag="woven%d" % i, align_bytes=64) for i in range(PIECES)]
 
         def cast(u, c, on_vector):
             lo = sum(CHUNKS[u][:c])
@@ -68,32 +71,51 @@ def tile_picked_edgeatt_sigmoid_e_kernel(tc, xT, w1, w2, w3, offs, src, dst, out
             else:
                 nc.scalar.copy(out=target, in_=source)
 
-        def pick(u):
-            nc.vector.tensor_copy(out=picked[:, :, u], in_=pairs[u][:].indirect(offs_sb[:]))
+        def pick(u, i):
+            nc.vector.tensor_copy(out=picked[i][:, u, :], in_=pairs[u][:].indirect(entries(offs_sb, i * PIECE, (i + 1) * PIECE)))
 
-        w_bf = [keep.tile([P, N, PACK], BF16, name="w_bf%d" % i, tag="staged%d" % i, align_bytes=64) for i in range(3)]
-        x_codes = keep.tile([P, S], U32, name="x_codes", tag="staged0", align_bytes=64)
-        x_scales = keep.tile([P, S], U8, name="x_scales", align_bytes=64)
+        def weave(i, on_vector):
+            if on_vector:
+                nc.vector.tensor_copy(out=woven[i][:].bitcast(I32), in_=picked[i][:].bitcast(I32).rearrange("p u n -> p n u"))
+            else:
+                nc.scalar.copy(out=woven[i][:], in_=picked[i][:].rearrange("p u n -> p n u"))
 
-        def quantise_x(i):
-            lo, hi = PIECES[i]
+        groups = (((0, 0),), ((1, 0),), ((0, 1), (1, 1)), ((2, 0), (2, 1)))
+        tags = ("first_w", "w_bf1", "woven%d" % (PIECES - 1), "first_codes")
+        w_bf, w_codes, w_scales, place = {}, {}, {}, {}
+        for g, members in enumerate(groups):
+            for s, member in enumerate(members):
+                place[member] = (g, s)
+            w_codes[g] = keep.tile([P, len(members) * P], U32, name="w_codes%d" % g, tag=("first_codes" if g == 0 else "w_codes%d" % g), align_bytes=64)
+            w_scales[g] = keep.tile([P, len(members) * P], U8, name="w_scales%d" % g, align_bytes=64)
+
+        def group_w(g, on_vector):
+            members = groups[g]
+            w_bf[g] = keep.tile([P, len(members) * P, PACK], BF16, name="w_bf%d" % g, tag=tags[g], align_bytes=64)
+            for s, (i, b) in enumerate(members):
+                target = w_bf[g][:, s * P : (s + 1) * P, :].rearrange("p (c i) j -> p c j i", i=4)
+                source = w_raw[i][:, :, b * P : (b + 1) * P].rearrange("p j (c i) -> p c j i", i=4)
+                if on_vector:
+                    nc.vector.tensor_copy(out=target, in_=source)
+                else:
+                    nc.scalar.copy(out=target, in_=source)
+
+        def quantise_w(g):
             nc.vector.quantize_mx(
-                out=x_codes[:, lo:hi].bitcast(FP8X4),
-                scales=x_scales[:, lo:hi],
-                in_=picked[:, lo:hi, :].rearrange("p n u -> p (n u)").bitcast(BF16),
+                out=w_codes[g][:].bitcast(FP8X4),
+                scales=w_scales[g][:],
+                in_=w_bf[g][:].rearrange("p n j -> p (n j)"),
             )
 
-        w_codes = [keep.tile([P, N], U32, name="w_codes%d" % i, align_bytes=64) for i in range(3)]
-        w_scales = [keep.tile([P, N], U8, name="w_scales%d" % i, align_bytes=64) for i in range(3)]
+        x_codes = {}
+        x_scales = [keep.tile([P, BANK], U8, name="x_scales%d" % h, align_bytes=64) for h in range(2)]
 
-        def group_w(i):
-            nc.scalar.copy(out=w_bf[i][:], in_=w_raw[i][:].rearrange("p j n -> p n j"))
-
-        def quantise_w(i):
+        def quantise_x(i):
+            h, lo = divmod(i * PIECE, BANK)
             nc.vector.quantize_mx(
-                out=w_codes[i][:].bitcast(FP8X4),
-                scales=w_scales[i][:],
-                in_=w_bf[i][:].rearrange("p n j -> p (n j)"),
+                out=x_codes[h][:, lo : lo + PIECE].bitcast(FP8X4),
+                scales=x_scales[h][:, lo : lo + PIECE],
+                in_=woven[i][:].rearrange("p n u -> p (n u)").bitcast(BF16),
             )
 
         res = {}
@@ -101,41 +123,55 @@ def tile_picked_edgeatt_sigmoid_e_kernel(tc, xT, w1, w2, w3, offs, src, dst, out
             for b in range(2):
                 res[i, b] = keep.tile([P, S], F32, name="res%d_%d" % (i, b))
 
-        def product(i, b, lo, hi, on_vector=False):
-            acc = psum.tile([P, BANK], F32, name="acc")
-            cols = slice(b * P, (b + 1) * P)
+        def product(i, b, lo, hi, bank):
+            acc = psum.tile([P, BANK], F32, name="acc", tag="bank%d" % bank)
+            g, s = place[i, b]
+            cols = slice(s * P, (s + 1) * P)
+            h, first = divmod(lo, BANK)
+            nodes = slice(first, first + hi - lo)
             nc.tensor.matmul_mx(
                 out=acc[:, : hi - lo],
-                lhsT=w_codes[i][:, cols].bitcast(FP8X4),
-                lhsT_scale=w_scales[i][:, cols],
-                rhs=x_codes[:, lo:hi].bitcast(FP8X4),
-                rhs_scale=x_scales[:, lo:hi],
+                lhsT=w_codes[g][:, cols].bitcast(FP8X4),
+                lhsT_scale=w_scales[g][:, cols],
+                rhs=x_codes[h][:, nodes].bitcast(FP8X4),
+                rhs_scale=x_scales[h][:, nodes],
                 start=True,
                 stop=True,
             )
-            if on_vector:
-                nc.vector.tensor_copy(out=res[i, b][:, lo:hi], in_=acc[:, : hi - lo])
-            else:
-                nc.scalar.copy(out=res[i, b][:, lo:hi], in_=acc[:, : hi - lo])
+            nc.scalar.copy(out=res[i, b][:, lo:hi], in_=acc[:, : hi - lo])
 
         for c in range(len(CHUNKS[0])):
             cast(0, c, True)
         for c in range(len(CHUNKS[1]) - 2):
             cast(1, c, False)
-        pick(0)
+        for i in range(PIECES):
+            pick(0, i)
         cast(1, len(CHUNKS[1]) - 2, True)
         cast(1, len(CHUNKS[1]) - 1, True)
-        pick(1)
-        group_w(0)
-        group_w(1)
-        group_w(2)
+        for i in range(PIECES):
+            pick(1, i)
+        weave(0, False)
+        group_w(0, False)
+        weave(1, False)
+        weave(2, False)
+        weave(3, True)
+        group_w(1, False)
+        x_codes[0] = keep.tile([P, BANK], U32, name="x_codes0", align_bytes=64)
+        quantise_x(0)
+        quantise_x(1)
         quantise_w(0)
-        for i in range(len(PIECES)):
-            quantise_x(i)
+        x_codes[1] = keep.tile([P, BANK], U32, name="x_codes1", tag="first_w", align_bytes=64)
+        quantise_x(2)
+        quantise_x(3)
         quantise_w(1)
-        for i in range(len(PIECES)):
-            product(0, 0, *PIECES[i])
+        group_w(2, True)
         quantise_w(2)
+        for i in range(PIECES):
+            product(0, 0, i * PIECE, (i + 1) * PIECE, i)
+        product(1, 0, *HALVES[1], 4)
+        product(1, 0, *HALVES[0], 2)
+        group_w(3, False)
+        quantise_w(3)
 
         y_dst = [keep.tile([P, U], F32, name="y_dst%d" % b) for b in range(2)]
         logit = [keep.tile([P, U], F32, name="logit%d" % b) for b in range(2)]
@@ -156,11 +192,16 @@ def tile_picked_edgeatt_sigmoid_e_kernel(tc, xT, w1, w2, w3, offs, src, dst, out
                 nc.vector.tensor_tensor(result[b][:, lo:hi], res[2, b][:].indirect(entries(src_sb, lo, hi)), gate[b][:, lo:hi], MULT)
                 nc.sync.dma_start(out=out[b * P : (b + 1) * P, lo:hi], in_=result[b][:, lo:hi])
 
-        for i, b in ((1, 0), (0, 1), (1, 1), (2, 0), (2, 1)):
-            for lo, hi in HALVES:
-                product(i, b, lo, hi)
+        product(0, 1, *HALVES[0], 5)
+        product(0, 1, *HALVES[1], 6)
+        product(1, 1, *HALVES[0], 7)
+        product(1, 1, *HALVES[1], 0)
         fetch_y(0)
         add_e(0)
+        product(2, 0, *HALVES[0], 1)
+        product(2, 0, *HALVES[1], 3)
+        product(2, 1, *HALVES[0], 4)
+        product(2, 1, *HALVES[1], 2)
         fetch_y(1)
         add_e(1)
         times_h(0, HALVES)

@@ -20,6 +20,7 @@ P = 128
 PACK = 4
 BANK = 512
 CHUNKS = ((1024, 512, 512), (512, 512, 512, 256, 256))
+SPARE = (384, 16, 16)
 PIECE = 256
 PIECES = S // PIECE
 HALVES = ((0, 512), (512, 1024))
@@ -80,7 +81,7 @@ def tile_picked_edgeatt_sigmoid_e_kernel(tc, xT, w1, w2, w3, offs, src, dst, out
             else:
                 nc.scalar.copy(out=woven[i][:], in_=picked[i][:].rearrange("p u n -> p n u"))
 
-        groups = (((0, 0),), ((1, 0),), ((0, 1), (1, 1)), ((2, 0), (2, 1)))
+        groups = (((0, 0),), ((0, 1),), ((1, 0), (1, 1)), ((2, 0), (2, 1)))
         tags = ("first_w", "w_bf1", "woven%d" % (PIECES - 1), "first_codes")
         w_bf, w_codes, w_scales, place = {}, {}, {}, {}
         for g, members in enumerate(groups):
@@ -92,13 +93,13 @@ def tile_picked_edgeatt_sigmoid_e_kernel(tc, xT, w1, w2, w3, offs, src, dst, out
         def group_w(g, on_vector):
             members = groups[g]
             w_bf[g] = keep.tile([P, len(members) * P, PACK], BF16, name="w_bf%d" % g, tag=tags[g], align_bytes=64)
-            for s, (i, b) in enumerate(members):
-                target = w_bf[g][:, s * P : (s + 1) * P, :].rearrange("p (c i) j -> p c j i", i=4)
-                source = w_raw[i][:, :, b * P : (b + 1) * P].rearrange("p j (c i) -> p c j i", i=4)
-                if on_vector:
-                    nc.vector.tensor_copy(out=target, in_=source)
-                else:
-                    nc.scalar.copy(out=target, in_=source)
+            i, b = members[0]
+            target = w_bf[g][:].rearrange("p (c i) j -> p c j i", i=4)
+            source = w_raw[i][:, :, b * P : (b + len(members)) * P].rearrange("p j (c i) -> p c j i", i=4)
+            if on_vector:
+                nc.vector.tensor_copy(out=target, in_=source)
+            else:
+                nc.scalar.copy(out=target, in_=source)
 
         def quantise_w(g):
             nc.vector.quantize_mx(
@@ -121,7 +122,11 @@ def tile_picked_edgeatt_sigmoid_e_kernel(tc, xT, w1, w2, w3, offs, src, dst, out
         res = {}
         for i in range(3):
             for b in range(2):
-                res[i, b] = keep.tile([P, S], F32, name="res%d_%d" % (i, b))
+                res[i, b] = keep.tile([P, S + SPARE[i]], F32, name="res%d_%d" % (i, b))
+                nc.gpsimd.memset(res[i, b][:, S:], 0.0)
+
+        warm = keep.tile([P, 1], F32, name="warm")
+        nc.scalar.activation(warm[:], res[0, 0][:, S : S + 1], SIGMOID)
 
         def product(i, b, lo, hi, bank):
             acc = psum.tile([P, BANK], F32, name="acc", tag="bank%d" % bank)
@@ -168,10 +173,10 @@ def tile_picked_edgeatt_sigmoid_e_kernel(tc, xT, w1, w2, w3, offs, src, dst, out
         quantise_w(2)
         for i in range(PIECES):
             product(0, 0, i * PIECE, (i + 1) * PIECE, i)
-        product(1, 0, *HALVES[1], 4)
-        product(1, 0, *HALVES[0], 2)
         group_w(3, False)
         quantise_w(3)
+        product(0, 1, *HALVES[1], 4)
+        product(0, 1, *HALVES[0], 2)
 
         y_dst = [keep.tile([P, U], F32, name="y_dst%d" % b) for b in range(2)]
         logit = [keep.tile([P, U], F32, name="logit%d" % b) for b in range(2)]
@@ -179,12 +184,12 @@ def tile_picked_edgeatt_sigmoid_e_kernel(tc, xT, w1, w2, w3, offs, src, dst, out
         result = [keep.tile([P, U], F32, name="result%d" % b) for b in range(2)]
 
         def fetch_y(b):
-            for lo, hi in HALVES:
-                nc.vector.tensor_copy(out=y_dst[b][:, lo:hi], in_=res[0, b][:].indirect(entries(dst_sb, lo, hi)))
+            nc.vector.tensor_copy(out=y_dst[b][:], in_=res[0, b][:].indirect(dst_sb[:]))
 
         def add_e(b):
-            for lo, hi in HALVES:
-                nc.vector.tensor_tensor(logit[b][:, lo:hi], res[1, b][:].indirect(entries(src_sb, lo, hi)), y_dst[b][:, lo:hi], ADD)
+            nc.vector.tensor_tensor(logit[b][:], res[1, b][:].indirect(src_sb[:]), y_dst[b][:], ADD)
+
+        def squash(b):
             nc.scalar.activation(gate[b][:], logit[b][:], SIGMOID)
 
         def times_h(b, cuts):
@@ -192,17 +197,19 @@ def tile_picked_edgeatt_sigmoid_e_kernel(tc, xT, w1, w2, w3, offs, src, dst, out
                 nc.vector.tensor_tensor(result[b][:, lo:hi], res[2, b][:].indirect(entries(src_sb, lo, hi)), gate[b][:, lo:hi], MULT)
                 nc.sync.dma_start(out=out[b * P : (b + 1) * P, lo:hi], in_=result[b][:, lo:hi])
 
-        product(0, 1, *HALVES[0], 5)
-        product(0, 1, *HALVES[1], 6)
+        product(1, 0, *HALVES[0], 5)
+        product(1, 0, *HALVES[1], 6)
         product(1, 1, *HALVES[0], 7)
         product(1, 1, *HALVES[1], 0)
-        fetch_y(0)
-        add_e(0)
         product(2, 0, *HALVES[0], 1)
         product(2, 0, *HALVES[1], 3)
+        fetch_y(0)
+        fetch_y(1)
+        add_e(0)
+        squash(0)
         product(2, 1, *HALVES[0], 4)
         product(2, 1, *HALVES[1], 2)
-        fetch_y(1)
         add_e(1)
-        times_h(0, HALVES)
+        squash(1)
+        times_h(0, ((0, U),))
         times_h(1, LAST)

@@ -19,12 +19,14 @@ SIGMOID = mybir.ActivationFunctionType.Sigmoid
 P = 128
 PACK = 4
 BANK = 512
-CHUNKS = ((1024, 512, 512), (512, 512, 512, 256, 256))
+CHUNKS = ((1024, 512, 512), (512, 512, 512, 384, 128))
+ON_VECTOR = ((1024, 512, 320), (0, 0, 320, 384, 0))
 SPARE = (384, 16, 16)
 PIECE = 256
 PIECES = S // PIECE
+NODE_CUTS = ((0, 256), (256, 512), (512, 768), (768, 896), (896, 1024))
 HALVES = ((0, 512), (512, 1024))
-LAST = ((0, 512), (512, 896), (896, 1024))
+LAST = ((0, 640), (640, 896), (896, 1024))
 
 
 def entries(offsets, lo, hi):
@@ -49,24 +51,30 @@ def tile_picked_edgeatt_sigmoid_e_kernel(tc, xT, w1, w2, w3, offs, src, dst, out
                 raw[u, c] = keep.tile([P, 2, width], F32, name="raw%d_%d" % (u, c))
                 nc.sync.dma_start(out=raw[u, c][:], in_=x_rows[:, 2 * u : 2 * u + 2, lo : lo + width])
                 lo = lo + width
-                if (u, c) == (0, 1):
+                if (u, c) == (0, 0):
                     nc.sync.dma_start(offs_sb[:], offs)
-        w_raw = []
+        w_raw = {}
         for i, w in enumerate((w1, w2, w3)):
-            w_raw.append(keep.tile([P, PACK, N], F32, name="w_raw%d" % i))
-            nc.sync.dma_start(out=w_raw[i][:], in_=w.rearrange("(p j) n -> p j n", j=PACK))
+            rows = w.rearrange("(p j) n -> p j n", j=PACK)
+            for lo, hi in ((0, P), (P, N)) if i == 0 else ((0, N),):
+                tile = keep.tile([P, PACK, hi - lo], F32, name="w_raw%d_%d" % (i, lo))
+                nc.sync.dma_start(out=tile[:], in_=rows[:, :, lo:hi])
+                for first in range(lo, hi, P):
+                    w_raw[i, first] = (tile, first - lo)
         nc.sync.dma_start(dst_sb[:], dst)
         nc.sync.dma_start(src_sb[:], src)
 
         pairs = [keep.tile([P, T], U32, name="pairs%d" % u, align_bytes=64) for u in range(2)]
-        picked = [keep.tile([P, 2, PIECE], U32, name="picked%d" % i, align_bytes=64) for i in range(PIECES)]
+        picked = [keep.tile([P, 2, PIECE], U32, name="picked%d" % i, tag="picked%d" % i, align_bytes=64) for i in range(PIECES)]
         woven = [keep.tile([P, PIECE, 2], U32, name="woven%d" % i, tag="woven%d" % i, align_bytes=64) for i in range(PIECES)]
 
         def cast(u, c, on_vector):
+            first, last = (0, ON_VECTOR[u][c]) if on_vector else (ON_VECTOR[u][c], CHUNKS[u][c])
+            if first == last:
+                return
             lo = sum(CHUNKS[u][:c])
-            width = CHUNKS[u][c]
-            target = pairs[u][:, lo : lo + width].bitcast(BF16).rearrange("p (t e) -> p t e", e=2)
-            source = raw[u, c][:].rearrange("p e t -> p t e")
+            target = pairs[u][:, lo + first : lo + last].bitcast(BF16).rearrange("p (t e) -> p t e", e=2)
+            source = raw[u, c][:, :, first:last].rearrange("p e t -> p t e")
             if on_vector:
                 nc.vector.tensor_copy(out=target, in_=source)
             else:
@@ -81,42 +89,39 @@ def tile_picked_edgeatt_sigmoid_e_kernel(tc, xT, w1, w2, w3, offs, src, dst, out
             else:
                 nc.scalar.copy(out=woven[i][:], in_=picked[i][:].rearrange("p u n -> p n u"))
 
-        groups = (((0, 0),), ((0, 1),), ((1, 0), (1, 1)), ((2, 0), (2, 1)))
-        tags = ("first_w", "w_bf1", "woven%d" % (PIECES - 1), "first_codes")
-        w_bf, w_codes, w_scales, place = {}, {}, {}, {}
-        for g, members in enumerate(groups):
-            for s, member in enumerate(members):
-                place[member] = (g, s)
-            w_codes[g] = keep.tile([P, len(members) * P], U32, name="w_codes%d" % g, tag=("first_codes" if g == 0 else "w_codes%d" % g), align_bytes=64)
-            w_scales[g] = keep.tile([P, len(members) * P], U8, name="w_scales%d" % g, align_bytes=64)
+        w_codes, w_scales, w_bf = {}, {}, {}
 
-        def group_w(g, on_vector):
-            members = groups[g]
-            w_bf[g] = keep.tile([P, len(members) * P, PACK], BF16, name="w_bf%d" % g, tag=tags[g], align_bytes=64)
-            i, b = members[0]
-            target = w_bf[g][:].rearrange("p (c i) j -> p c j i", i=4)
-            source = w_raw[i][:, :, b * P : (b + len(members)) * P].rearrange("p j (c i) -> p c j i", i=4)
+        def weight_tiles(name, members, bf_tag, codes_tag):
+            bf = keep.tile([P, len(members) * P, PACK], BF16, name="w_bf_" + name, tag=bf_tag, align_bytes=64)
+            codes = keep.tile([P, len(members) * P], U32, name="w_codes_" + name, tag=codes_tag, align_bytes=64)
+            scales = keep.tile([P, len(members) * P], U8, name="w_scales_" + name, align_bytes=64)
+            for s, member in enumerate(members):
+                cols = slice(s * P, (s + 1) * P)
+                w_bf[member], w_codes[member], w_scales[member] = bf[:, cols, :], codes[:, cols], scales[:, cols]
+            return bf, codes, scales
+
+        def regroup(target, i, lo, hi, on_vector):
+            target = target.rearrange("p (c i) j -> p c j i", i=4)
+            tile, first = w_raw[i, lo]
+            source = tile[:, :, first : first + hi - lo].rearrange("p j (c i) -> p c j i", i=4)
             if on_vector:
                 nc.vector.tensor_copy(out=target, in_=source)
             else:
                 nc.scalar.copy(out=target, in_=source)
 
-        def quantise_w(g):
-            nc.vector.quantize_mx(
-                out=w_codes[g][:].bitcast(FP8X4),
-                scales=w_scales[g][:],
-                in_=w_bf[g][:].rearrange("p n j -> p (n j)"),
-            )
+        def quantise_w(bf, codes, scales):
+            nc.vector.quantize_mx(out=codes.bitcast(FP8X4), scales=scales, in_=bf.rearrange("p n j -> p (n j)"))
 
-        x_codes = {}
+        x_codes = [keep.tile([P, BANK], U32, name="x_codes%d" % h, align_bytes=64) for h in range(2)]
         x_scales = [keep.tile([P, BANK], U8, name="x_scales%d" % h, align_bytes=64) for h in range(2)]
 
-        def quantise_x(i):
-            h, lo = divmod(i * PIECE, BANK)
+        def quantise_x(lo, hi):
+            h, first = divmod(lo, BANK)
+            i, start = divmod(lo, PIECE)
             nc.vector.quantize_mx(
-                out=x_codes[h][:, lo : lo + PIECE].bitcast(FP8X4),
-                scales=x_scales[h][:, lo : lo + PIECE],
-                in_=woven[i][:].rearrange("p n u -> p (n u)").bitcast(BF16),
+                out=x_codes[h][:, first : first + hi - lo].bitcast(FP8X4),
+                scales=x_scales[h][:, first : first + hi - lo],
+                in_=woven[i][:, start : start + hi - lo, :].rearrange("p n u -> p (n u)").bitcast(BF16),
             )
 
         res = {}
@@ -130,53 +135,18 @@ def tile_picked_edgeatt_sigmoid_e_kernel(tc, xT, w1, w2, w3, offs, src, dst, out
 
         def product(i, b, lo, hi, bank):
             acc = psum.tile([P, BANK], F32, name="acc", tag="bank%d" % bank)
-            g, s = place[i, b]
-            cols = slice(s * P, (s + 1) * P)
             h, first = divmod(lo, BANK)
             nodes = slice(first, first + hi - lo)
             nc.tensor.matmul_mx(
                 out=acc[:, : hi - lo],
-                lhsT=w_codes[g][:, cols].bitcast(FP8X4),
-                lhsT_scale=w_scales[g][:, cols],
+                lhsT=w_codes[i, b].bitcast(FP8X4),
+                lhsT_scale=w_scales[i, b],
                 rhs=x_codes[h][:, nodes].bitcast(FP8X4),
                 rhs_scale=x_scales[h][:, nodes],
                 start=True,
                 stop=True,
             )
             nc.scalar.copy(out=res[i, b][:, lo:hi], in_=acc[:, : hi - lo])
-
-        for c in range(len(CHUNKS[0])):
-            cast(0, c, True)
-        for c in range(len(CHUNKS[1]) - 2):
-            cast(1, c, False)
-        for i in range(PIECES):
-            pick(0, i)
-        cast(1, len(CHUNKS[1]) - 2, True)
-        cast(1, len(CHUNKS[1]) - 1, True)
-        for i in range(PIECES):
-            pick(1, i)
-        weave(0, False)
-        group_w(0, False)
-        weave(1, False)
-        weave(2, False)
-        weave(3, True)
-        group_w(1, False)
-        x_codes[0] = keep.tile([P, BANK], U32, name="x_codes0", align_bytes=64)
-        quantise_x(0)
-        quantise_x(1)
-        quantise_w(0)
-        x_codes[1] = keep.tile([P, BANK], U32, name="x_codes1", tag="first_w", align_bytes=64)
-        quantise_x(2)
-        quantise_x(3)
-        quantise_w(1)
-        group_w(2, True)
-        quantise_w(2)
-        for i in range(PIECES):
-            product(0, 0, i * PIECE, (i + 1) * PIECE, i)
-        group_w(3, False)
-        quantise_w(3)
-        product(0, 1, *HALVES[1], 4)
-        product(0, 1, *HALVES[0], 2)
 
         y_dst = [keep.tile([P, U], F32, name="y_dst%d" % b) for b in range(2)]
         logit = [keep.tile([P, U], F32, name="logit%d" % b) for b in range(2)]
@@ -197,18 +167,54 @@ def tile_picked_edgeatt_sigmoid_e_kernel(tc, xT, w1, w2, w3, offs, src, dst, out
                 nc.vector.tensor_tensor(result[b][:, lo:hi], res[2, b][:].indirect(entries(src_sb, lo, hi)), gate[b][:, lo:hi], MULT)
                 nc.sync.dma_start(out=out[b * P : (b + 1) * P, lo:hi], in_=result[b][:, lo:hi])
 
-        product(1, 0, *HALVES[0], 5)
-        product(1, 0, *HALVES[1], 6)
-        product(1, 1, *HALVES[0], 7)
-        product(1, 1, *HALVES[1], 0)
-        product(2, 0, *HALVES[0], 1)
-        product(2, 0, *HALVES[1], 3)
+        for c in range(len(CHUNKS[0])):
+            cast(0, c, True)
+            cast(0, c, False)
+        for i in range(PIECES):
+            pick(0, i)
+        for c in range(len(CHUNKS[1])):
+            cast(1, c, True)
+            cast(1, c, False)
+        for i in range(PIECES):
+            pick(1, i)
+        first = weight_tiles("first", ((0, 0),), "w_bf_first", "first_codes")
+        regroup(first[0][:], 0, 0, P, False)
+        for i in range(PIECES):
+            weave(i, False)
+        quantise_w(first[0][:], first[1][:], first[2][:])
+        for cut in NODE_CUTS:
+            quantise_x(*cut)
+        for i, cut in enumerate(NODE_CUTS):
+            product(0, 0, *cut, i)
+
+        weight_tiles("second", ((0, 1), (1, 0)), "picked%d" % (PIECES - 1), "second_codes")
+        w_codes[0, 1] = keep.tile([P, P], U32, name="y1_codes", tag="y1_codes", align_bytes=64)[:]
+        regroup(w_bf[0, 1], 0, P, N, True)
+        regroup(w_bf[1, 0], 1, 0, P, True)
+        quantise_w(w_bf[0, 1], w_codes[0, 1], w_scales[0, 1])
+        quantise_w(w_bf[1, 0], w_codes[1, 0], w_scales[1, 0])
         fetch_y(0)
+
+        third = weight_tiles("third", ((1, 1),), "first_codes", "third_codes")
+        regroup(third[0][:], 1, P, N, False)
+        quantise_w(third[0][:], third[1][:], third[2][:])
+        product(0, 1, *HALVES[0], 5)
+        product(0, 1, *HALVES[1], 6)
+        fourth = weight_tiles("fourth", ((2, 0), (2, 1)), "y1_codes", "fourth_codes")
+        regroup(fourth[0][:], 2, 0, N, False)
         fetch_y(1)
+        quantise_w(fourth[0][:], fourth[1][:], fourth[2][:])
+
+        product(1, 0, *HALVES[0], 7)
+        product(1, 0, *HALVES[1], 0)
+        product(1, 1, *HALVES[0], 1)
+        product(1, 1, *HALVES[1], 2)
+        product(2, 0, *HALVES[0], 3)
+        product(2, 0, *HALVES[1], 4)
+        product(2, 1, *HALVES[0], 5)
+        product(2, 1, *HALVES[1], 6)
         add_e(0)
         squash(0)
-        product(2, 1, *HALVES[0], 4)
-        product(2, 1, *HALVES[1], 2)
         add_e(1)
         squash(1)
         times_h(0, ((0, U),))

@@ -20,7 +20,7 @@ P = 128
 PACK = 4
 BANK = 512
 CHUNKS = ((1024, 512, 512), (512, 512, 512, 384, 128))
-ON_VECTOR = ((1024, 512, 320), (0, 0, 320, 384, 0))
+ON_VECTOR = ((704, 352, 352), (0, 0, 320, 384, 0))
 SPARE = (384, 16, 16)
 PIECE = 256
 PIECES = S // PIECE
@@ -45,14 +45,19 @@ def tile_picked_edgeatt_sigmoid_e_kernel(tc, xT, w1, w2, w3, offs, src, dst, out
         dst_sb = keep.tile([P, U // 16], U16, name="dst_sb")
 
         raw = {}
+        whole = keep.tile([P, 2, T], F32, name="raw0")
+        nc.sync.dma_start(out=whole[:, 0, :], in_=x_rows[:, 0, :])
+        nc.sync.dma_start(offs_sb[:], offs)
         for u in range(2):
             lo = 0
             for c, width in enumerate(CHUNKS[u]):
-                raw[u, c] = keep.tile([P, 2, width], F32, name="raw%d_%d" % (u, c))
-                nc.sync.dma_start(out=raw[u, c][:], in_=x_rows[:, 2 * u : 2 * u + 2, lo : lo + width])
+                if u == 0:
+                    raw[u, c] = (whole, lo)
+                    nc.sync.dma_start(out=whole[:, 1, lo : lo + width], in_=x_rows[:, 1, lo : lo + width])
+                else:
+                    raw[u, c] = (keep.tile([P, 2, width], F32, name="raw1_%d" % c), 0)
+                    nc.sync.dma_start(out=raw[u, c][0][:], in_=x_rows[:, 2:4, lo : lo + width])
                 lo = lo + width
-                if (u, c) == (0, 0):
-                    nc.sync.dma_start(offs_sb[:], offs)
         w_raw = {}
         for i, w in enumerate((w1, w2, w3)):
             rows = w.rearrange("(p j) n -> p j n", j=PACK)
@@ -74,7 +79,8 @@ def tile_picked_edgeatt_sigmoid_e_kernel(tc, xT, w1, w2, w3, offs, src, dst, out
                 return
             lo = sum(CHUNKS[u][:c])
             target = pairs[u][:, lo + first : lo + last].bitcast(BF16).rearrange("p (t e) -> p t e", e=2)
-            source = raw[u, c][:, :, first:last].rearrange("p e t -> p t e")
+            tile, start = raw[u, c]
+            source = tile[:, :, start + first : start + last].rearrange("p e t -> p t e")
             if on_vector:
                 nc.vector.tensor_copy(out=target, in_=source)
             else:
@@ -211,10 +217,10 @@ def tile_picked_edgeatt_sigmoid_e_kernel(tc, xT, w1, w2, w3, offs, src, dst, out
         product(1, 1, *HALVES[1], 2)
         product(2, 0, *HALVES[0], 3)
         product(2, 0, *HALVES[1], 4)
-        product(2, 1, *HALVES[0], 5)
-        product(2, 1, *HALVES[1], 6)
         add_e(0)
         squash(0)
+        product(2, 1, *HALVES[0], 5)
+        product(2, 1, *HALVES[1], 6)
         add_e(1)
         squash(1)
         times_h(0, ((0, U),))

@@ -19,8 +19,8 @@ SIGMOID = mybir.ActivationFunctionType.Sigmoid
 P = 128
 PACK = 4
 BANK = 512
-CHUNKS = ((1024, 512, 512), (512, 512, 512, 384, 128))
-ON_VECTOR = ((704, 352, 352), (0, 0, 320, 384, 0))
+CHUNKS = ((1408, 640), (1024, 768, 256))
+ON_VECTOR = ((896, 432), (432, 496, 176))
 SPARE = (384, 16, 16)
 PIECE = 256
 PIECES = S // PIECE
@@ -45,19 +45,14 @@ def tile_picked_edgeatt_sigmoid_e_kernel(tc, xT, w1, w2, w3, offs, src, dst, out
         dst_sb = keep.tile([P, U // 16], U16, name="dst_sb")
 
         raw = {}
-        whole = keep.tile([P, 2, T], F32, name="raw0")
-        nc.sync.dma_start(out=whole[:, 0, :], in_=x_rows[:, 0, :])
-        nc.sync.dma_start(offs_sb[:], offs)
         for u in range(2):
             lo = 0
             for c, width in enumerate(CHUNKS[u]):
-                if u == 0:
-                    raw[u, c] = (whole, lo)
-                    nc.sync.dma_start(out=whole[:, 1, lo : lo + width], in_=x_rows[:, 1, lo : lo + width])
-                else:
-                    raw[u, c] = (keep.tile([P, 2, width], F32, name="raw1_%d" % c), 0)
-                    nc.sync.dma_start(out=raw[u, c][0][:], in_=x_rows[:, 2:4, lo : lo + width])
+                raw[u, c] = keep.tile([P, 2, width], F32, name="raw%d_%d" % (u, c))
+                nc.sync.dma_start(out=raw[u, c][:], in_=x_rows[:, 2 * u : 2 * u + 2, lo : lo + width])
                 lo = lo + width
+            if u == 0:
+                nc.sync.dma_start(offs_sb[:], offs)
         w_raw = {}
         for i, w in enumerate((w1, w2, w3)):
             rows = w.rearrange("(p j) n -> p j n", j=PACK)
@@ -79,8 +74,7 @@ def tile_picked_edgeatt_sigmoid_e_kernel(tc, xT, w1, w2, w3, offs, src, dst, out
                 return
             lo = sum(CHUNKS[u][:c])
             target = pairs[u][:, lo + first : lo + last].bitcast(BF16).rearrange("p (t e) -> p t e", e=2)
-            tile, start = raw[u, c]
-            source = tile[:, :, start + first : start + last].rearrange("p e t -> p t e")
+            source = raw[u, c][:, :, first:last].rearrange("p e t -> p t e")
             if on_vector:
                 nc.vector.tensor_copy(out=target, in_=source)
             else:

@@ -19,14 +19,14 @@ SIGMOID = mybir.ActivationFunctionType.Sigmoid
 P = 128
 PACK = 4
 BANK = 512
-CHUNKS = ((1408, 640), (1024, 768, 256))
-ON_VECTOR = ((896, 432), (432, 496, 176))
+CHUNKS = ((1408, 640), (1152, 704, 192))
+ON_VECTOR = ((896, 432), (544, 448, 128))
 SPARE = (384, 16, 16)
 PIECE = 256
 PIECES = S // PIECE
 NODE_CUTS = ((0, 256), (256, 512), (512, 768), (768, 896), (896, 1024))
 HALVES = ((0, 512), (512, 1024))
-LAST = ((0, 640), (640, 896), (896, 1024))
+LAST = ((0, 544), (544, 832), (832, 1024))
 
 
 def entries(offsets, lo, hi):
@@ -83,11 +83,10 @@ def tile_picked_edgeatt_sigmoid_e_kernel(tc, xT, w1, w2, w3, offs, src, dst, out
         def pick(u, i):
             nc.vector.tensor_copy(out=picked[i][:, u, :], in_=pairs[u][:].indirect(entries(offs_sb, i * PIECE, (i + 1) * PIECE)))
 
-        def weave(i, on_vector):
-            if on_vector:
-                nc.vector.tensor_copy(out=woven[i][:].bitcast(I32), in_=picked[i][:].bitcast(I32).rearrange("p u n -> p n u"))
-            else:
-                nc.scalar.copy(out=woven[i][:], in_=picked[i][:].rearrange("p u n -> p n u"))
+        def weave(lo, hi):
+            i, start = divmod(lo, PIECE)
+            nodes = slice(start, start + hi - lo)
+            nc.scalar.copy(out=woven[i][:, nodes, :], in_=picked[i][:, :, nodes].rearrange("p u n -> p n u"))
 
         w_codes, w_scales, w_bf = {}, {}, {}
 
@@ -179,8 +178,8 @@ def tile_picked_edgeatt_sigmoid_e_kernel(tc, xT, w1, w2, w3, offs, src, dst, out
             pick(1, i)
         first = weight_tiles("first", ((0, 0),), "w_bf_first", "first_codes")
         regroup(first[0][:], 0, 0, P, False)
-        for i in range(PIECES):
-            weave(i, False)
+        for cut in NODE_CUTS:
+            weave(*cut)
         quantise_w(first[0][:], first[1][:], first[2][:])
         for cut in NODE_CUTS:
             quantise_x(*cut)

@@ -19,14 +19,14 @@ SIGMOID = mybir.ActivationFunctionType.Sigmoid
 P = 128
 PACK = 4
 BANK = 512
-CHUNKS = ((1408, 640), (1152, 704, 192))
-ON_VECTOR = ((896, 432), (544, 448, 128))
+CHUNKS = ((1408, 640), (1360, 560, 128))
+ON_VECTOR = ((896, 432), (832, 400, 0))
 SPARE = (384, 16, 16)
 PIECE = 256
 PIECES = S // PIECE
 NODE_CUTS = ((0, 256), (256, 512), (512, 768), (768, 896), (896, 1024))
 HALVES = ((0, 512), (512, 1024))
-LAST = ((0, 544), (544, 832), (832, 1024))
+LAST = ((0, 576), (576, 864), (864, 1024))
 
 
 def entries(offsets, lo, hi):

@@ -7,7 +7,6 @@ FLOPS = 3 * 2 * K * N * S
 
 F32 = mybir.dt.float32
 BF16 = mybir.dt.bfloat16
-I32 = mybir.dt.int32
 U32 = mybir.dt.uint32
 U16 = mybir.dt.uint16
 U8 = mybir.dt.uint8
@@ -15,18 +14,16 @@ FP8X4 = mybir.dt.float8_e4m3fn_x4
 ADD = mybir.AluOpType.add
 MULT = mybir.AluOpType.mult
 SIGMOID = mybir.ActivationFunctionType.Sigmoid
+COPY = mybir.ActivationFunctionType.Copy
 
 P = 128
 PACK = 4
 BANK = 512
-CHUNKS = ((1408, 640), (1360, 560, 128))
-ON_VECTOR = ((896, 432), (832, 400, 0))
-SPARE = (384, 16, 16)
+SPARE = 16
 PIECE = 256
 PIECES = S // PIECE
-NODE_CUTS = ((0, 256), (256, 512), (512, 768), (768, 896), (896, 1024))
 HALVES = ((0, 512), (512, 1024))
-LAST = ((0, 576), (576, 864), (864, 1024))
+FUSED = 768
 
 
 def entries(offsets, lo, hi):
@@ -44,95 +41,86 @@ def tile_picked_edgeatt_sigmoid_e_kernel(tc, xT, w1, w2, w3, offs, src, dst, out
         src_sb = keep.tile([P, U // 16], U16, name="src_sb")
         dst_sb = keep.tile([P, U // 16], U16, name="dst_sb")
 
-        raw = {}
-        for u in range(2):
-            lo = 0
-            for c, width in enumerate(CHUNKS[u]):
-                raw[u, c] = keep.tile([P, 2, width], F32, name="raw%d_%d" % (u, c))
-                nc.sync.dma_start(out=raw[u, c][:], in_=x_rows[:, 2 * u : 2 * u + 2, lo : lo + width])
-                lo = lo + width
-            if u == 0:
+        row = []
+        for j in range(PACK):
+            row.append(keep.tile([P, T], F32, name="row%d" % j))
+            nc.sync.dma_start(out=row[j][:], in_=x_rows[:, j, :])
+            if j == 0:
                 nc.sync.dma_start(offs_sb[:], offs)
+
         w_raw = {}
-        for i, w in enumerate((w1, w2, w3)):
-            rows = w.rearrange("(p j) n -> p j n", j=PACK)
-            for lo, hi in ((0, P), (P, N)) if i == 0 else ((0, N),):
-                tile = keep.tile([P, PACK, hi - lo], F32, name="w_raw%d_%d" % (i, lo))
-                nc.sync.dma_start(out=tile[:], in_=rows[:, :, lo:hi])
-                for first in range(lo, hi, P):
-                    w_raw[i, first] = (tile, first - lo)
+
+        def load_w(i, w, lo, hi):
+            tile = keep.tile([P, PACK, hi - lo], F32, name="w_raw%d_%d" % (i, lo))
+            nc.sync.dma_start(out=tile[:], in_=w.rearrange("(p j) n -> p j n", j=PACK)[:, :, lo:hi])
+            for first in range(lo, hi, P):
+                w_raw[i, first // P] = tile[:, :, first - lo : first - lo + P]
+
+        load_w(0, w1, 0, P)
+        load_w(1, w2, 0, N)
         nc.sync.dma_start(dst_sb[:], dst)
+        load_w(0, w1, P, N)
         nc.sync.dma_start(src_sb[:], src)
+        load_w(2, w3, 0, N)
 
-        pairs = [keep.tile([P, T], U32, name="pairs%d" % u, align_bytes=64) for u in range(2)]
-        picked = [keep.tile([P, 2, PIECE], U32, name="picked%d" % i, tag="picked%d" % i, align_bytes=64) for i in range(PIECES)]
-        woven = [keep.tile([P, PIECE, 2], U32, name="woven%d" % i, tag="woven%d" % i, align_bytes=64) for i in range(PIECES)]
+        low = keep.tile([P, 2, S], BF16, name="low", align_bytes=64)
+        high = {i: keep.tile([P, 2, PIECE], BF16, name="high%d" % i, align_bytes=64) for i in range(1, PIECES)}
+        woven = [keep.tile([P, PIECE, PACK], BF16, name="woven%d" % i, tag="woven%d" % i, align_bytes=64) for i in range(PIECES)]
 
-        def cast(u, c, on_vector):
-            first, last = (0, ON_VECTOR[u][c]) if on_vector else (ON_VECTOR[u][c], CHUNKS[u][c])
-            if first == last:
-                return
-            lo = sum(CHUNKS[u][:c])
-            target = pairs[u][:, lo + first : lo + last].bitcast(BF16).rearrange("p (t e) -> p t e", e=2)
-            source = raw[u, c][:, :, first:last].rearrange("p e t -> p t e")
+        def pick(target, j, lo, hi, on_vector):
+            window = row[j][:].indirect(entries(offs_sb, lo, hi))
             if on_vector:
-                nc.vector.tensor_copy(out=target, in_=source)
+                nc.vector.tensor_copy(out=target, in_=window)
             else:
-                nc.scalar.copy(out=target, in_=source)
+                nc.scalar.activation(target, window, COPY)
 
-        def pick(u, i):
-            nc.vector.tensor_copy(out=picked[i][:, u, :], in_=pairs[u][:].indirect(entries(offs_sb, i * PIECE, (i + 1) * PIECE)))
-
-        def weave(lo, hi):
-            i, start = divmod(lo, PIECE)
-            nodes = slice(start, start + hi - lo)
-            nc.scalar.copy(out=woven[i][:, nodes, :], in_=picked[i][:, :, nodes].rearrange("p u n -> p n u"))
+        def weave(i, first, planes):
+            nc.vector.tensor_copy(out=woven[i][:, :, first : first + 2], in_=planes.rearrange("p e n -> p n e"))
 
         w_codes, w_scales, w_bf = {}, {}, {}
 
-        def weight_tiles(name, members, bf_tag, codes_tag):
+        def weight_tiles(name, members, bf_tag):
             bf = keep.tile([P, len(members) * P, PACK], BF16, name="w_bf_" + name, tag=bf_tag, align_bytes=64)
-            codes = keep.tile([P, len(members) * P], U32, name="w_codes_" + name, tag=codes_tag, align_bytes=64)
+            codes = keep.tile([P, len(members) * P], U32, name="w_codes_" + name, align_bytes=64)
             scales = keep.tile([P, len(members) * P], U8, name="w_scales_" + name, align_bytes=64)
             for s, member in enumerate(members):
                 cols = slice(s * P, (s + 1) * P)
                 w_bf[member], w_codes[member], w_scales[member] = bf[:, cols, :], codes[:, cols], scales[:, cols]
             return bf, codes, scales
 
-        def regroup(target, i, lo, hi, on_vector):
-            target = target.rearrange("p (c i) j -> p c j i", i=4)
-            tile, first = w_raw[i, lo]
-            source = tile[:, :, first : first + hi - lo].rearrange("p j (c i) -> p c j i", i=4)
+        def regroup(member, on_vector):
+            target = w_bf[member].rearrange("p (c i) j -> p c j i", i=4)
+            source = w_raw[member].rearrange("p j (c i) -> p c j i", i=4)
             if on_vector:
                 nc.vector.tensor_copy(out=target, in_=source)
             else:
                 nc.scalar.copy(out=target, in_=source)
 
         def quantise_w(bf, codes, scales):
-            nc.vector.quantize_mx(out=codes.bitcast(FP8X4), scales=scales, in_=bf.rearrange("p n j -> p (n j)"))
+            nc.vector.quantize_mx(out=codes[:].bitcast(FP8X4), scales=scales[:], in_=bf[:].rearrange("p n j -> p (n j)"))
 
         x_codes = [keep.tile([P, BANK], U32, name="x_codes%d" % h, align_bytes=64) for h in range(2)]
         x_scales = [keep.tile([P, BANK], U8, name="x_scales%d" % h, align_bytes=64) for h in range(2)]
 
-        def quantise_x(lo, hi):
-            h, first = divmod(lo, BANK)
-            i, start = divmod(lo, PIECE)
+        def quantise_x(i):
+            h, first = divmod(i * PIECE, BANK)
             nc.vector.quantize_mx(
-                out=x_codes[h][:, first : first + hi - lo].bitcast(FP8X4),
-                scales=x_scales[h][:, first : first + hi - lo],
-                in_=woven[i][:, start : start + hi - lo, :].rearrange("p n u -> p (n u)").bitcast(BF16),
+                out=x_codes[h][:, first : first + PIECE].bitcast(FP8X4),
+                scales=x_scales[h][:, first : first + PIECE],
+                in_=woven[i][:].rearrange("p n j -> p (n j)"),
             )
 
         res = {}
         for i in range(3):
             for b in range(2):
-                res[i, b] = keep.tile([P, S + SPARE[i]], F32, name="res%d_%d" % (i, b))
-                nc.gpsimd.memset(res[i, b][:, S:], 0.0)
+                spare = SPARE if (i, b) == (2, 0) else 0
+                res[i, b] = keep.tile([P, S + spare], F32, name="res%d_%d" % (i, b))
+        nc.gpsimd.memset(res[2, 0][:, S:], 0.0)
 
         warm = keep.tile([P, 1], F32, name="warm")
-        nc.scalar.activation(warm[:], res[0, 0][:, S : S + 1], SIGMOID)
+        nc.scalar.activation(warm[:], res[2, 0][:, S : S + 1], SIGMOID)
 
-        def product(i, b, lo, hi, bank):
+        def product(i, b, lo, hi, bank, on_vector):
             acc = psum.tile([P, BANK], F32, name="acc", tag="bank%d" % bank)
             h, first = divmod(lo, BANK)
             nodes = slice(first, first + hi - lo)
@@ -145,76 +133,100 @@ def tile_picked_edgeatt_sigmoid_e_kernel(tc, xT, w1, w2, w3, offs, src, dst, out
                 start=True,
                 stop=True,
             )
-            nc.scalar.copy(out=res[i, b][:, lo:hi], in_=acc[:, : hi - lo])
+            if on_vector:
+                nc.vector.tensor_copy(out=res[i, b][:, lo:hi], in_=acc[:, : hi - lo])
+            else:
+                nc.scalar.copy(out=res[i, b][:, lo:hi], in_=acc[:, : hi - lo])
 
         y_dst = [keep.tile([P, U], F32, name="y_dst%d" % b) for b in range(2)]
         logit = [keep.tile([P, U], F32, name="logit%d" % b) for b in range(2)]
         gate = [keep.tile([P, U], F32, name="gate%d" % b) for b in range(2)]
         result = [keep.tile([P, U], F32, name="result%d" % b) for b in range(2)]
+        h_src = keep.tile([P, U - FUSED], F32, name="h_src")
 
-        def fetch_y(b):
-            nc.vector.tensor_copy(out=y_dst[b][:], in_=res[0, b][:].indirect(dst_sb[:]))
+        def fetch_y(b, lo, hi):
+            nc.scalar.activation(y_dst[b][:, lo:hi], res[0, b][:].indirect(entries(dst_sb, lo, hi)), COPY)
 
-        def add_e(b):
-            nc.vector.tensor_tensor(logit[b][:], res[1, b][:].indirect(src_sb[:]), y_dst[b][:], ADD)
+        def add_e(b, lo, hi):
+            nc.vector.tensor_tensor(logit[b][:, lo:hi], res[1, b][:].indirect(entries(src_sb, lo, hi)), y_dst[b][:, lo:hi], ADD)
 
-        def squash(b):
-            nc.scalar.activation(gate[b][:], logit[b][:], SIGMOID)
+        def squash(b, lo, hi):
+            nc.scalar.activation(gate[b][:, lo:hi], logit[b][:, lo:hi], SIGMOID)
 
-        def times_h(b, cuts):
-            for lo, hi in cuts:
-                nc.vector.tensor_tensor(result[b][:, lo:hi], res[2, b][:].indirect(entries(src_sb, lo, hi)), gate[b][:, lo:hi], MULT)
-                nc.sync.dma_start(out=out[b * P : (b + 1) * P, lo:hi], in_=result[b][:, lo:hi])
+        def store(b, lo, hi):
+            nc.sync.dma_start(out=out[b * P : (b + 1) * P, lo:hi], in_=result[b][:, lo:hi])
 
-        for c in range(len(CHUNKS[0])):
-            cast(0, c, True)
-            cast(0, c, False)
+        def times_h(b, lo, hi):
+            nc.vector.tensor_tensor(result[b][:, lo:hi], res[2, b][:].indirect(entries(src_sb, lo, hi)), gate[b][:, lo:hi], MULT)
+
+        def nodes(i):
+            return i * PIECE, (i + 1) * PIECE
+
+        pick(low[:, 0, :], 0, 0, S, False)
+        pick(low[:, 1, :BANK], 1, 0, BANK, True)
+        pick(low[:, 1, BANK:], 1, BANK, S, False)
         for i in range(PIECES):
-            pick(0, i)
-        for c in range(len(CHUNKS[1])):
-            cast(1, c, True)
-            cast(1, c, False)
-        for i in range(PIECES):
-            pick(1, i)
-        first = weight_tiles("first", ((0, 0),), "w_bf_first", "first_codes")
-        regroup(first[0][:], 0, 0, P, False)
-        for cut in NODE_CUTS:
-            weave(*cut)
-        quantise_w(first[0][:], first[1][:], first[2][:])
-        for cut in NODE_CUTS:
-            quantise_x(*cut)
-        for i, cut in enumerate(NODE_CUTS):
-            product(0, 0, *cut, i)
+            weave(i, 0, low[:, :, i * PIECE : (i + 1) * PIECE])
+        pick(woven[0][:, :, 2], 2, *nodes(0), True)
+        for i in range(1, PIECES):
+            pick(high[i][:, 0, :], 2, *nodes(i), False)
 
-        weight_tiles("second", ((0, 1), (1, 0)), "picked%d" % (PIECES - 1), "second_codes")
-        w_codes[0, 1] = keep.tile([P, P], U32, name="y1_codes", tag="y1_codes", align_bytes=64)[:]
-        regroup(w_bf[0, 1], 0, P, N, True)
-        regroup(w_bf[1, 0], 1, 0, P, True)
-        quantise_w(w_bf[0, 1], w_codes[0, 1], w_scales[0, 1])
-        quantise_w(w_bf[1, 0], w_codes[1, 0], w_scales[1, 0])
-        fetch_y(0)
+        y0 = weight_tiles("y0", ((0, 0),), "y0_bf")
+        e0 = weight_tiles("e0", ((1, 0),), "e0_bf")
+        pick(woven[0][:, :, 3], 3, *nodes(0), True)
+        pick(high[1][:, 1, :], 3, *nodes(1), False)
+        pick(high[2][:, 1, :], 3, *nodes(2), False)
+        regroup((0, 0), False)
+        pick(high[3][:, 1, :], 3, *nodes(3), False)
+        regroup((1, 0), False)
+        weave(1, 2, high[1][:])
+        quantise_x(0)
+        weave(2, 2, high[2][:])
+        quantise_x(1)
+        quantise_w(*y0)
+        weave(3, 2, high[3][:])
+        quantise_x(2)
+        quantise_w(*e0)
+        quantise_x(3)
+        product(0, 0, 0, 512, 0, False)
+        product(0, 0, 512, 768, 2, False)
+        product(1, 0, 0, 512, 1, False)
+        product(0, 0, 768, 1024, 6, False)
+        for half in HALVES:
+            fetch_y(0, *half)
 
-        third = weight_tiles("third", ((1, 1),), "first_codes", "third_codes")
-        regroup(third[0][:], 1, P, N, False)
-        quantise_w(third[0][:], third[1][:], third[2][:])
-        product(0, 1, *HALVES[0], 5)
-        product(0, 1, *HALVES[1], 6)
-        fourth = weight_tiles("fourth", ((2, 0), (2, 1)), "y1_codes", "fourth_codes")
-        regroup(fourth[0][:], 2, 0, N, False)
-        fetch_y(1)
-        quantise_w(fourth[0][:], fourth[1][:], fourth[2][:])
-
-        product(1, 0, *HALVES[0], 7)
-        product(1, 0, *HALVES[1], 0)
-        product(1, 1, *HALVES[0], 1)
-        product(1, 1, *HALVES[1], 2)
-        product(2, 0, *HALVES[0], 3)
-        product(2, 0, *HALVES[1], 4)
-        add_e(0)
-        squash(0)
-        product(2, 1, *HALVES[0], 5)
-        product(2, 1, *HALVES[1], 6)
-        add_e(1)
-        squash(1)
-        times_h(0, ((0, U),))
-        times_h(1, LAST)
+        second = weight_tiles("second", ((0, 1), (2, 0)), "woven2")
+        third = weight_tiles("third", ((1, 1), (2, 1)), "woven3")
+        regroup((0, 1), True)
+        regroup((2, 0), True)
+        regroup((1, 1), True)
+        quantise_w(*second)
+        regroup((2, 1), True)
+        product(1, 0, 512, 1024, 3, True)
+        quantise_w(*third)
+        product(0, 1, *HALVES[0], 6, False)
+        product(0, 1, *HALVES[1], 3, False)
+        for half in HALVES:
+            add_e(0, *half)
+            squash(0, *half)
+        product(2, 0, *HALVES[0], 4, True)
+        product(2, 0, *HALVES[1], 5, True)
+        product(1, 1, *HALVES[0], 6, False)
+        product(1, 1, *HALVES[1], 3, False)
+        times_h(0, 0, U)
+        store(0, 0, U)
+        for half in HALVES:
+            fetch_y(1, *half)
+        product(2, 1, *HALVES[0], 6, False)
+        product(2, 1, *HALVES[1], 3, False)
+        add_e(1, *HALVES[0])
+        squash(1, *HALVES[0])
+        nc.scalar.activation(h_src[:], res[2, 1][:].indirect(entries(src_sb, FUSED, U)), COPY)
+        add_e(1, *HALVES[1])
+        squash(1, *HALVES[1])
+        times_h(1, *HALVES[0])
+        store(1, *HALVES[0])
+        times_h(1, BANK, FUSED)
+        store(1, BANK, FUSED)
+        nc.vector.tensor_tensor(result[1][:, FUSED:], h_src[:], gate[1][:, FUSED:], MULT)
+        store(1, FUSED, U)

@@ -19,15 +19,23 @@ COPY = mybir.ActivationFunctionType.Copy
 P = 128
 PACK = 4
 BANK = 512
-SPARE = 16
+STRIPE = 16
+Y, E, H = 0, 1, 2
+HALVES = ((0, BANK), (BANK, 2 * BANK))
+
 PIECE = 256
 PIECES = S // PIECE
-HALVES = ((0, 512), (512, 1024))
-FUSED = 768
+
+FUSED = 480
+FETCHED = ((FUSED, 864), (864, U))
 
 
 def entries(offsets, lo, hi):
-    return offsets[:, lo // 16 : hi // 16]
+    return offsets[:, lo // STRIPE : hi // STRIPE]
+
+
+def nodes(i):
+    return i * PIECE, (i + 1) * PIECE
 
 
 def tile_picked_edgeatt_sigmoid_e_kernel(tc, xT, w1, w2, w3, offs, src, dst, out):
@@ -37,9 +45,9 @@ def tile_picked_edgeatt_sigmoid_e_kernel(tc, xT, w1, w2, w3, offs, src, dst, out
         psum = ctx.enter_context(tc.psum_pool(name="psum", bufs=1))
 
         x_rows = xT.rearrange("(p j) t -> p j t", j=PACK)
-        offs_sb = keep.tile([P, S // 16], U16, name="offs_sb")
-        src_sb = keep.tile([P, U // 16], U16, name="src_sb")
-        dst_sb = keep.tile([P, U // 16], U16, name="dst_sb")
+        offs_sb = keep.tile([P, S // STRIPE], U16, name="offs_sb")
+        src_sb = keep.tile([P, U // STRIPE], U16, name="src_sb")
+        dst_sb = keep.tile([P, U // STRIPE], U16, name="dst_sb")
 
         row = []
         for j in range(PACK):
@@ -48,95 +56,91 @@ def tile_picked_edgeatt_sigmoid_e_kernel(tc, xT, w1, w2, w3, offs, src, dst, out
             if j == 0:
                 nc.sync.dma_start(offs_sb[:], offs)
 
-        w_raw = {}
-
-        def load_w(i, w, lo, hi):
-            tile = keep.tile([P, PACK, hi - lo], F32, name="w_raw%d_%d" % (i, lo))
+        def load_w(name, w, lo, hi):
+            tile = keep.tile([P, PACK, hi - lo], F32, name=name)
             nc.sync.dma_start(out=tile[:], in_=w.rearrange("(p j) n -> p j n", j=PACK)[:, :, lo:hi])
-            for first in range(lo, hi, P):
-                w_raw[i, first // P] = tile[:, :, first - lo : first - lo + P]
+            return tile
 
-        load_w(0, w1, 0, P)
-        load_w(1, w2, 0, N)
+        w1_first = load_w("w1_first", w1, 0, P)
+        w2_raw = load_w("w2_raw", w2, 0, N)
+        w1_second = load_w("w1_second", w1, P, N)
+        w3_raw = load_w("w3_raw", w3, 0, N)
         nc.sync.dma_start(dst_sb[:], dst)
-        load_w(0, w1, P, N)
         nc.sync.dma_start(src_sb[:], src)
-        load_w(2, w3, 0, N)
 
         low = keep.tile([P, 2, S], BF16, name="low", align_bytes=64)
         high = {i: keep.tile([P, 2, PIECE], BF16, name="high%d" % i, align_bytes=64) for i in range(1, PIECES)}
         woven = [keep.tile([P, PIECE, PACK], BF16, name="woven%d" % i, tag="woven%d" % i, align_bytes=64) for i in range(PIECES)]
 
-        def pick(target, j, lo, hi, on_vector):
-            window = row[j][:].indirect(entries(offs_sb, lo, hi))
+        def gather(target, window, on_vector):
             if on_vector:
                 nc.vector.tensor_copy(out=target, in_=window)
             else:
                 nc.scalar.activation(target, window, COPY)
 
-        def weave(i, first, planes):
-            nc.vector.tensor_copy(out=woven[i][:, :, first : first + 2], in_=planes.rearrange("p e n -> p n e"))
+        def pick(target, j, lo, hi, on_vector):
+            gather(target, row[j][:].indirect(entries(offs_sb, lo, hi)), on_vector)
 
-        w_codes, w_scales, w_bf = {}, {}, {}
+        def weave(i, first, two_rows):
+            nc.vector.tensor_copy(out=woven[i][:, :, first : first + 2], in_=two_rows.rearrange("p e n -> p n e"))
 
-        def weight_tiles(name, members, bf_tag):
-            bf = keep.tile([P, len(members) * P, PACK], BF16, name="w_bf_" + name, tag=bf_tag, align_bytes=64)
+        w_codes, w_scales = {}, {}
+
+        def weight_tiles(name, members, tag):
+            grouped = keep.tile([P, len(members) * P, PACK], BF16, name="w_grouped_" + name, tag=tag, align_bytes=64)
             codes = keep.tile([P, len(members) * P], U32, name="w_codes_" + name, align_bytes=64)
             scales = keep.tile([P, len(members) * P], U8, name="w_scales_" + name, align_bytes=64)
-            for s, member in enumerate(members):
-                cols = slice(s * P, (s + 1) * P)
-                w_bf[member], w_codes[member], w_scales[member] = bf[:, cols, :], codes[:, cols], scales[:, cols]
-            return bf, codes, scales
+            for place, member in enumerate(members):
+                cols = slice(place * P, (place + 1) * P)
+                w_codes[member], w_scales[member] = codes[:, cols], scales[:, cols]
+            return grouped, codes, scales
 
-        def regroup(member, on_vector):
-            target = w_bf[member].rearrange("p (c i) j -> p c j i", i=4)
-            source = w_raw[member].rearrange("p j (c i) -> p c j i", i=4)
+        def regroup(grouped, raw, on_vector):
+            target = grouped[:].rearrange("p (c i) j -> p c j i", i=4)
+            source = raw.rearrange("p j (c i) -> p c j i", i=4)
             if on_vector:
                 nc.vector.tensor_copy(out=target, in_=source)
             else:
                 nc.scalar.copy(out=target, in_=source)
 
-        def quantise_w(bf, codes, scales):
-            nc.vector.quantize_mx(out=codes[:].bitcast(FP8X4), scales=scales[:], in_=bf[:].rearrange("p n j -> p (n j)"))
+        def quantise_w(grouped, codes, scales):
+            nc.vector.quantize_mx(out=codes[:].bitcast(FP8X4), scales=scales[:], in_=grouped[:].rearrange("p n j -> p (n j)"))
 
-        x_codes = [keep.tile([P, BANK], U32, name="x_codes%d" % h, align_bytes=64) for h in range(2)]
-        x_scales = [keep.tile([P, BANK], U8, name="x_scales%d" % h, align_bytes=64) for h in range(2)]
+        x_codes = [keep.tile([P, BANK], U32, name="x_codes%d" % half, align_bytes=64) for half in range(2)]
+        x_scales = [keep.tile([P, BANK], U8, name="x_scales%d" % half, align_bytes=64) for half in range(2)]
 
         def quantise_x(i):
-            h, first = divmod(i * PIECE, BANK)
+            half, first = divmod(i * PIECE, BANK)
             nc.vector.quantize_mx(
-                out=x_codes[h][:, first : first + PIECE].bitcast(FP8X4),
-                scales=x_scales[h][:, first : first + PIECE],
+                out=x_codes[half][:, first : first + PIECE].bitcast(FP8X4),
+                scales=x_scales[half][:, first : first + PIECE],
                 in_=woven[i][:].rearrange("p n j -> p (n j)"),
             )
 
         res = {}
-        for i in range(3):
+        for m in (Y, E, H):
             for b in range(2):
-                spare = SPARE if (i, b) == (2, 0) else 0
-                res[i, b] = keep.tile([P, S + spare], F32, name="res%d_%d" % (i, b))
-        nc.gpsimd.memset(res[2, 0][:, S:], 0.0)
+                spare = STRIPE if (m, b) == (E, 0) else 0
+                res[m, b] = keep.tile([P, S + spare], F32, name="res%d_%d" % (m, b))
+        nc.gpsimd.memset(res[E, 0][:, S:], 0.0)
 
         warm = keep.tile([P, 1], F32, name="warm")
-        nc.scalar.activation(warm[:], res[2, 0][:, S : S + 1], SIGMOID)
+        nc.scalar.activation(warm[:], res[E, 0][:, S : S + 1], SIGMOID)
 
-        def product(i, b, lo, hi, bank, on_vector):
+        def product(m, b, lo, hi, bank):
             acc = psum.tile([P, BANK], F32, name="acc", tag="bank%d" % bank)
-            h, first = divmod(lo, BANK)
-            nodes = slice(first, first + hi - lo)
+            half, first = divmod(lo, BANK)
+            cols = slice(first, first + hi - lo)
             nc.tensor.matmul_mx(
                 out=acc[:, : hi - lo],
-                lhsT=w_codes[i, b].bitcast(FP8X4),
-                lhsT_scale=w_scales[i, b],
-                rhs=x_codes[h][:, nodes].bitcast(FP8X4),
-                rhs_scale=x_scales[h][:, nodes],
+                lhsT=w_codes[m, b].bitcast(FP8X4),
+                lhsT_scale=w_scales[m, b],
+                rhs=x_codes[half][:, cols].bitcast(FP8X4),
+                rhs_scale=x_scales[half][:, cols],
                 start=True,
                 stop=True,
             )
-            if on_vector:
-                nc.vector.tensor_copy(out=res[i, b][:, lo:hi], in_=acc[:, : hi - lo])
-            else:
-                nc.scalar.copy(out=res[i, b][:, lo:hi], in_=acc[:, : hi - lo])
+            nc.scalar.copy(out=res[m, b][:, lo:hi], in_=acc[:, : hi - lo])
 
         y_dst = [keep.tile([P, U], F32, name="y_dst%d" % b) for b in range(2)]
         logit = [keep.tile([P, U], F32, name="logit%d" % b) for b in range(2)]
@@ -144,89 +148,84 @@ def tile_picked_edgeatt_sigmoid_e_kernel(tc, xT, w1, w2, w3, offs, src, dst, out
         result = [keep.tile([P, U], F32, name="result%d" % b) for b in range(2)]
         h_src = keep.tile([P, U - FUSED], F32, name="h_src")
 
-        def fetch_y(b, lo, hi):
-            nc.scalar.activation(y_dst[b][:, lo:hi], res[0, b][:].indirect(entries(dst_sb, lo, hi)), COPY)
+        def fetch_y(b, lo, hi, on_vector):
+            gather(y_dst[b][:, lo:hi], res[Y, b][:].indirect(entries(dst_sb, lo, hi)), on_vector)
 
         def add_e(b, lo, hi):
-            nc.vector.tensor_tensor(logit[b][:, lo:hi], res[1, b][:].indirect(entries(src_sb, lo, hi)), y_dst[b][:, lo:hi], ADD)
+            nc.vector.tensor_tensor(logit[b][:, lo:hi], res[E, b][:].indirect(entries(src_sb, lo, hi)), y_dst[b][:, lo:hi], ADD)
 
         def squash(b, lo, hi):
             nc.scalar.activation(gate[b][:, lo:hi], logit[b][:, lo:hi], SIGMOID)
 
+        def times_h(b, lo, hi):
+            nc.vector.tensor_tensor(result[b][:, lo:hi], res[H, b][:].indirect(entries(src_sb, lo, hi)), gate[b][:, lo:hi], MULT)
+
         def store(b, lo, hi):
             nc.sync.dma_start(out=out[b * P : (b + 1) * P, lo:hi], in_=result[b][:, lo:hi])
 
-        def times_h(b, lo, hi):
-            nc.vector.tensor_tensor(result[b][:, lo:hi], res[2, b][:].indirect(entries(src_sb, lo, hi)), gate[b][:, lo:hi], MULT)
-
-        def nodes(i):
-            return i * PIECE, (i + 1) * PIECE
-
-        pick(low[:, 0, :], 0, 0, S, False)
-        pick(low[:, 1, :BANK], 1, 0, BANK, True)
-        pick(low[:, 1, BANK:], 1, BANK, S, False)
+        for j in range(2):
+            pick(low[:, j, :BANK], j, 0, BANK, True)
+            pick(low[:, j, BANK:], j, BANK, S, False)
         for i in range(PIECES):
             weave(i, 0, low[:, :, i * PIECE : (i + 1) * PIECE])
         pick(woven[0][:, :, 2], 2, *nodes(0), True)
         for i in range(1, PIECES):
             pick(high[i][:, 0, :], 2, *nodes(i), False)
 
-        y0 = weight_tiles("y0", ((0, 0),), "y0_bf")
-        e0 = weight_tiles("e0", ((1, 0),), "e0_bf")
+        y0 = weight_tiles("y0", ((Y, 0),), "y0")
+        e0 = weight_tiles("e0", ((E, 0),), "e0")
+        y1 = weight_tiles("y1", ((Y, 1),), "y1")
         pick(woven[0][:, :, 3], 3, *nodes(0), True)
-        pick(high[1][:, 1, :], 3, *nodes(1), False)
-        pick(high[2][:, 1, :], 3, *nodes(2), False)
-        regroup((0, 0), False)
-        pick(high[3][:, 1, :], 3, *nodes(3), False)
-        regroup((1, 0), False)
+        for i in range(1, PIECES):
+            pick(high[i][:, 1, :], 3, *nodes(i), False)
+        regroup(y0[0], w1_first[:], True)
+        regroup(e0[0], w2_raw[:, :, :P], False)
+        regroup(y1[0], w1_second[:], False)
         weave(1, 2, high[1][:])
         quantise_x(0)
+        quantise_w(*y0)
         weave(2, 2, high[2][:])
         quantise_x(1)
-        quantise_w(*y0)
         weave(3, 2, high[3][:])
         quantise_x(2)
-        quantise_w(*e0)
         quantise_x(3)
-        product(0, 0, 0, 512, 0, False)
-        product(0, 0, 512, 768, 2, False)
-        product(1, 0, 0, 512, 1, False)
-        product(0, 0, 768, 1024, 6, False)
-        for half in HALVES:
-            fetch_y(0, *half)
+        quantise_w(*e0)
+        quantise_w(*y1)
+        e1 = weight_tiles("e1", ((E, 1),), "woven2")
+        h = weight_tiles("h", ((H, 0), (H, 1)), "woven3")
+        regroup(e1[0], w2_raw[:, :, P:], True)
+        regroup(h[0], w3_raw[:], True)
+        quantise_w(*e1)
+        quantise_w(*h)
 
-        second = weight_tiles("second", ((0, 1), (2, 0)), "woven2")
-        third = weight_tiles("third", ((1, 1), (2, 1)), "woven3")
-        regroup((0, 1), True)
-        regroup((2, 0), True)
-        regroup((1, 1), True)
-        quantise_w(*second)
-        regroup((2, 1), True)
-        product(1, 0, 512, 1024, 3, True)
-        quantise_w(*third)
-        product(0, 1, *HALVES[0], 6, False)
-        product(0, 1, *HALVES[1], 3, False)
+        for i in range(PIECES):
+            product(Y, 0, *nodes(i), i)
         for half in HALVES:
-            add_e(0, *half)
+            fetch_y(0, *half, True)
+        product(E, 0, *HALVES[0], 4)
+        product(E, 0, *HALVES[1], 5)
+        product(Y, 1, *HALVES[0], 6)
+        product(Y, 1, *HALVES[1], 7)
+        product(E, 1, *HALVES[0], 0)
+        fetch_y(1, *HALVES[0], False)
+        product(E, 1, *HALVES[1], 1)
+        add_e(0, 0, U)
+        fetch_y(1, *HALVES[1], False)
+        product(H, 0, *HALVES[0], 2)
+        product(H, 0, *HALVES[1], 3)
+        for half in HALVES:
+            add_e(1, *half)
+        for half in HALVES:
             squash(0, *half)
-        product(2, 0, *HALVES[0], 4, True)
-        product(2, 0, *HALVES[1], 5, True)
-        product(1, 1, *HALVES[0], 6, False)
-        product(1, 1, *HALVES[1], 3, False)
-        times_h(0, 0, U)
-        store(0, 0, U)
-        for half in HALVES:
-            fetch_y(1, *half)
-        product(2, 1, *HALVES[0], 6, False)
-        product(2, 1, *HALVES[1], 3, False)
-        add_e(1, *HALVES[0])
-        squash(1, *HALVES[0])
-        nc.scalar.activation(h_src[:], res[2, 1][:].indirect(entries(src_sb, FUSED, U)), COPY)
-        add_e(1, *HALVES[1])
-        squash(1, *HALVES[1])
-        times_h(1, *HALVES[0])
-        store(1, *HALVES[0])
-        times_h(1, BANK, FUSED)
-        store(1, BANK, FUSED)
-        nc.vector.tensor_tensor(result[1][:, FUSED:], h_src[:], gate[1][:, FUSED:], MULT)
-        store(1, FUSED, U)
+            times_h(0, *half)
+            store(0, *half)
+        product(H, 1, *HALVES[0], 4)
+        product(H, 1, *HALVES[1], 5)
+        squash(1, 0, U)
+        for lo, hi in FETCHED:
+            gather(h_src[:, lo - FUSED : hi - FUSED], res[H, 1][:].indirect(entries(src_sb, lo, hi)), False)
+        times_h(1, 0, FUSED)
+        store(1, 0, FUSED)
+        for lo, hi in FETCHED:
+            nc.vector.tensor_tensor(result[1][:, lo:hi], h_src[:, lo - FUSED : hi - FUSED], gate[1][:, lo:hi], MULT)
+            store(1, lo, hi)

@@ -26,8 +26,8 @@ HALVES = ((0, BANK), (BANK, 2 * BANK))
 PIECE = 256
 PIECES = S // PIECE
 
-FUSED = 480
-FETCHED = ((FUSED, 864), (864, U))
+FUSED = 448
+FETCHED = ((FUSED, 832), (832, U))
 
 
 def entries(offsets, lo, hi):
@@ -190,13 +190,13 @@ def tile_picked_edgeatt_sigmoid_e_kernel(tc, xT, w1, w2, w3, offs, src, dst, out
         quantise_x(2)
         quantise_x(3)
         quantise_w(*e0)
-        quantise_w(*y1)
-        e1 = weight_tiles("e1", ((E, 1),), "woven2")
-        h = weight_tiles("h", ((H, 0), (H, 1)), "woven3")
-        regroup(e1[0], w2_raw[:, :, P:], True)
+        e1 = weight_tiles("e1", ((E, 1),), "woven3")
+        h = weight_tiles("h", ((H, 0), (H, 1)), "woven2")
         regroup(h[0], w3_raw[:], True)
-        quantise_w(*e1)
+        regroup(e1[0], w2_raw[:, :, P:], True)
+        quantise_w(*y1)
         quantise_w(*h)
+        quantise_w(*e1)
 
         for i in range(PIECES):
             product(Y, 0, *nodes(i), i)

@@ -26,7 +26,7 @@ HALVES = ((0, BANK), (BANK, 2 * BANK))
 PIECE = 256
 PIECES = S // PIECE
 
-FUSED = 448
+FUSED = 512
 FETCHED = ((FUSED, 832), (832, U))
 
 
@@ -127,7 +127,7 @@ def tile_picked_edgeatt_sigmoid_e_kernel(tc, xT, w1, w2, w3, offs, src, dst, out
         warm = keep.tile([P, 1], F32, name="warm")
         nc.scalar.activation(warm[:], res[E, 0][:, S : S + 1], SIGMOID)
 
-        def product(m, b, lo, hi, bank):
+        def product(m, b, lo, hi, bank, on_vector=False):
             acc = psum.tile([P, BANK], F32, name="acc", tag="bank%d" % bank)
             half, first = divmod(lo, BANK)
             cols = slice(first, first + hi - lo)
@@ -140,7 +140,10 @@ def tile_picked_edgeatt_sigmoid_e_kernel(tc, xT, w1, w2, w3, offs, src, dst, out
                 start=True,
                 stop=True,
             )
-            nc.scalar.copy(out=res[m, b][:, lo:hi], in_=acc[:, : hi - lo])
+            if on_vector:
+                nc.vector.tensor_copy(out=res[m, b][:, lo:hi], in_=acc[:, : hi - lo])
+            else:
+                nc.scalar.copy(out=res[m, b][:, lo:hi], in_=acc[:, : hi - lo])
 
         y_dst = [keep.tile([P, U], F32, name="y_dst%d" % b) for b in range(2)]
         logit = [keep.tile([P, U], F32, name="logit%d" % b) for b in range(2)]
@@ -190,18 +193,18 @@ def tile_picked_edgeatt_sigmoid_e_kernel(tc, xT, w1, w2, w3, offs, src, dst, out
         quantise_x(2)
         quantise_x(3)
         quantise_w(*e0)
-        e1 = weight_tiles("e1", ((E, 1),), "woven3")
-        h = weight_tiles("h", ((H, 0), (H, 1)), "woven2")
-        regroup(h[0], w3_raw[:], True)
+        e1 = weight_tiles("e1", ((E, 1),), "woven2")
         regroup(e1[0], w2_raw[:, :, P:], True)
         quantise_w(*y1)
-        quantise_w(*h)
         quantise_w(*e1)
+        h = weight_tiles("h", ((H, 0), (H, 1)), "woven2")
+        nc.gpsimd.tensor_scalar(h[0][:], w3_raw[:].rearrange("p j n -> p n j"), 1.0, 0.0, MULT, ADD)
 
         for i in range(PIECES):
-            product(Y, 0, *nodes(i), i)
+            product(Y, 0, *nodes(i), i, i == 2)
         for half in HALVES:
             fetch_y(0, *half, True)
+        quantise_w(*h)
         product(E, 0, *HALVES[0], 4)
         product(E, 0, *HALVES[1], 5)
         product(Y, 1, *HALVES[0], 6)
@@ -221,7 +224,8 @@ def tile_picked_edgeatt_sigmoid_e_kernel(tc, xT, w1, w2, w3, offs, src, dst, out
             store(0, *half)
         product(H, 1, *HALVES[0], 4)
         product(H, 1, *HALVES[1], 5)
-        squash(1, 0, U)
+        squash(1, 0, FUSED)
+        squash(1, FUSED, U)
         for lo, hi in FETCHED:
             gather(h_src[:, lo - FUSED : hi - FUSED], res[H, 1][:].indirect(entries(src_sb, lo, hi)), False)
         times_h(1, 0, FUSED)

@@ -62,8 +62,8 @@ def tile_picked_edgeatt_sigmoid_e_kernel(tc, xT, w1, w2, w3, offs, src, dst, out
             return tile
 
         w1_first = load_w("w1_first", w1, 0, P)
-        w2_raw = load_w("w2_raw", w2, 0, N)
         w1_second = load_w("w1_second", w1, P, N)
+        w2_raw = load_w("w2_raw", w2, 0, N)
         w3_raw = load_w("w3_raw", w3, 0, N)
         nc.sync.dma_start(dst_sb[:], dst)
         nc.sync.dma_start(src_sb[:], src)
@@ -109,19 +109,18 @@ def tile_picked_edgeatt_sigmoid_e_kernel(tc, xT, w1, w2, w3, offs, src, dst, out
         x_codes = [keep.tile([P, BANK], U32, name="x_codes%d" % half, align_bytes=64) for half in range(2)]
         x_scales = [keep.tile([P, BANK], U8, name="x_scales%d" % half, align_bytes=64) for half in range(2)]
 
-        def quantise_x(i):
+        def quantise_x(i, lo=0, hi=PIECE):
             half, first = divmod(i * PIECE, BANK)
             nc.vector.quantize_mx(
-                out=x_codes[half][:, first : first + PIECE].bitcast(FP8X4),
-                scales=x_scales[half][:, first : first + PIECE],
-                in_=woven[i][:].rearrange("p n j -> p (n j)"),
+                out=x_codes[half][:, first + lo : first + hi].bitcast(FP8X4),
+                scales=x_scales[half][:, first + lo : first + hi],
+                in_=woven[i][:, lo:hi, :].rearrange("p n j -> p (n j)"),
             )
 
         res = {}
-        for m in (Y, E, H):
-            for b in range(2):
-                spare = STRIPE if (m, b) == (E, 0) else 0
-                res[m, b] = keep.tile([P, S + spare], F32, name="res%d_%d" % (m, b))
+        for m, b in ((E, 0), (E, 1), (H, 0), (H, 1)):
+            spare = STRIPE if (m, b) == (E, 0) else 0
+            res[m, b] = keep.tile([P, S + spare], F32, name="res%d_%d" % (m, b))
         nc.gpsimd.memset(res[E, 0][:, S:], 0.0)
 
         warm = keep.tile([P, 1], F32, name="warm")
@@ -176,60 +175,70 @@ def tile_picked_edgeatt_sigmoid_e_kernel(tc, xT, w1, w2, w3, offs, src, dst, out
             pick(high[i][:, 0, :], 2, *nodes(i), False)
 
         y0 = weight_tiles("y0", ((Y, 0),), "y0")
-        e0 = weight_tiles("e0", ((E, 0),), "e0")
         y1 = weight_tiles("y1", ((Y, 1),), "y1")
         pick(woven[0][:, :, 3], 3, *nodes(0), True)
-        for i in range(1, PIECES):
+        for i in range(1, PIECES - 1):
             pick(high[i][:, 1, :], 3, *nodes(i), False)
+        pick(high[3][:, 1, P:], 3, S - P, S, False)
+        pick(high[3][:, 1, :P], 3, S - PIECE, S - P, False)
+        nc.scalar.copy(out=woven[3][:, P:, 2:], in_=high[3][:, :, P:].rearrange("p e n -> p n e"))
+        nc.scalar.copy(out=woven[3][:, 64:P, 2:], in_=high[3][:, :, 64:P].rearrange("p e n -> p n e"))
         regroup(y0[0], w1_first[:], True)
-        regroup(e0[0], w2_raw[:, :, :P], False)
         regroup(y1[0], w1_second[:], False)
         weave(1, 2, high[1][:])
         quantise_x(0)
         quantise_w(*y0)
         weave(2, 2, high[2][:])
         quantise_x(1)
-        weave(3, 2, high[3][:])
         quantise_x(2)
-        quantise_x(3)
-        quantise_w(*e0)
-        e1 = weight_tiles("e1", ((E, 1),), "woven2")
-        regroup(e1[0], w2_raw[:, :, P:], True)
+        nc.vector.tensor_copy(out=woven[3][:, :64, 2:], in_=high[3][:, :, :64].rearrange("p e n -> p n e"))
+        quantise_x(3, P, PIECE)
+        quantise_x(3, 0, P)
         quantise_w(*y1)
+        e0 = weight_tiles("e0", ((E, 0),), "woven2")
+        e1 = weight_tiles("e1", ((E, 1),), "woven3")
+        regroup(e0[0], w2_raw[:, :, :P], True)
+        regroup(e1[0], w2_raw[:, :, P:], True)
+        quantise_w(*e0)
         quantise_w(*e1)
-        h = weight_tiles("h", ((H, 0), (H, 1)), "woven2")
+        h = weight_tiles("h", ((H, 0), (H, 1)), "woven3")
         nc.gpsimd.tensor_scalar(h[0][:], w3_raw[:].rearrange("p j n -> p n j"), 1.0, 0.0, MULT, ADD)
 
-        for i in range(PIECES):
+        res[Y, 0] = keep.tile([P, S], F32, name="res_y0", tag="w1_second")
+        for i in range(PIECES - 1):
             product(Y, 0, *nodes(i), i, i == 2)
+        product(Y, 0, S - P, S, 3)
+        product(Y, 0, S - PIECE, S - P, 4)
         for half in HALVES:
             fetch_y(0, *half, True)
         quantise_w(*h)
-        product(E, 0, *HALVES[0], 4)
-        product(E, 0, *HALVES[1], 5)
-        product(Y, 1, *HALVES[0], 6)
-        product(Y, 1, *HALVES[1], 7)
-        product(E, 1, *HALVES[0], 0)
+        res[Y, 1] = keep.tile([P, S], F32, name="res_y1", tag="w_codes_y0", align_bytes=64)
+        product(Y, 1, *HALVES[0], 5)
+        product(Y, 1, *HALVES[1], 6)
+        product(E, 0, *HALVES[0], 7)
+        product(E, 0, *HALVES[1], 0)
+        product(E, 1, *HALVES[0], 1)
         fetch_y(1, *HALVES[0], False)
-        product(E, 1, *HALVES[1], 1)
+        product(E, 1, *HALVES[1], 2)
         add_e(0, 0, U)
         fetch_y(1, *HALVES[1], False)
-        product(H, 0, *HALVES[0], 2)
-        product(H, 0, *HALVES[1], 3)
+        product(H, 0, *HALVES[0], 3)
+        product(H, 0, *HALVES[1], 4)
         for half in HALVES:
             add_e(1, *half)
         for half in HALVES:
             squash(0, *half)
             times_h(0, *half)
-            store(0, *half)
-        product(H, 1, *HALVES[0], 4)
-        product(H, 1, *HALVES[1], 5)
+        store(0, 0, U)
+        product(H, 1, *HALVES[0], 5)
+        product(H, 1, *HALVES[1], 6)
         squash(1, 0, FUSED)
         squash(1, FUSED, U)
         for lo, hi in FETCHED:
             gather(h_src[:, lo - FUSED : hi - FUSED], res[H, 1][:].indirect(entries(src_sb, lo, hi)), False)
-        times_h(1, 0, FUSED)
-        store(1, 0, FUSED)
+        for part in ((0, FUSED // 2), (FUSED // 2, FUSED)):
+            times_h(1, *part)
+            store(1, *part)
         for lo, hi in FETCHED:
             nc.vector.tensor_tensor(result[1][:, lo:hi], h_src[:, lo - FUSED : hi - FUSED], gate[1][:, lo:hi], MULT)
             store(1, lo, hi)

@@ -206,7 +206,18 @@ def tile_picked_edgeatt_sigmoid_e_kernel(tc, xT, w1, w2, w3, offs, src, dst, out
 
         res[Y, 0] = keep.tile([P, S], F32, name="res_y0", tag="w1_second")
         for i in range(PIECES - 1):
-            product(Y, 0, *nodes(i), i, i == 2)
+            product(Y, 0, *nodes(i), i)
+            if i == 0:
+                idle = psum.tile([P, BANK], F32, name="idle", tag="bank7")
+                nc.tensor.matmul_mx(
+                    out=idle[:, :PIECE],
+                    lhsT=w_codes[Y, 0].bitcast(FP8X4),
+                    lhsT_scale=w_scales[Y, 0],
+                    rhs=x_codes[0][:, :PIECE].bitcast(FP8X4),
+                    rhs_scale=x_scales[0][:, :PIECE],
+                    start=True,
+                    stop=True,
+                )
         product(Y, 0, S - P, S, 3)
         product(Y, 0, S - PIECE, S - P, 4)
         for half in HALVES:

@@ -207,17 +207,6 @@ def tile_picked_edgeatt_sigmoid_e_kernel(tc, xT, w1, w2, w3, offs, src, dst, out
         res[Y, 0] = keep.tile([P, S], F32, name="res_y0", tag="w1_second")
         for i in range(PIECES - 1):
             product(Y, 0, *nodes(i), i)
-            if i == 0:
-                idle = psum.tile([P, BANK], F32, name="idle", tag="bank7")
-                nc.tensor.matmul_mx(
-                    out=idle[:, :PIECE],
-                    lhsT=w_codes[Y, 0].bitcast(FP8X4),
-                    lhsT_scale=w_scales[Y, 0],
-                    rhs=x_codes[0][:, :PIECE].bitcast(FP8X4),
-                    rhs_scale=x_scales[0][:, :PIECE],
-                    start=True,
-                    stop=True,
-                )
         product(Y, 0, S - P, S, 3)
         product(Y, 0, S - PIECE, S - P, 4)
         for half in HALVES:

@@ -69,7 +69,7 @@ def tile_picked_edgeatt_sigmoid_e_kernel(tc, xT, w1, w2, w3, offs, src, dst, out
         nc.sync.dma_start(src_sb[:], src)
 
         low = keep.tile([P, 2, S], BF16, name="low", align_bytes=64)
-        high = {i: keep.tile([P, 2, PIECE], BF16, name="high%d" % i, align_bytes=64) for i in range(1, PIECES)}
+        high = {i: keep.tile([P, 2, PIECE], BF16, name="high%d" % i, align_bytes=64) for i in range(PIECES)}
         woven = [keep.tile([P, PIECE, PACK], BF16, name="woven%d" % i, tag="woven%d" % i, align_bytes=64) for i in range(PIECES)]
 
         def gather(target, window, on_vector):
@@ -170,13 +170,13 @@ def tile_picked_edgeatt_sigmoid_e_kernel(tc, xT, w1, w2, w3, offs, src, dst, out
             pick(low[:, j, BANK:], j, BANK, S, False)
         for i in range(PIECES):
             weave(i, 0, low[:, :, i * PIECE : (i + 1) * PIECE])
-        pick(woven[0][:, :, 2], 2, *nodes(0), True)
+        pick(high[0][:, 0, :], 2, *nodes(0), True)
         for i in range(1, PIECES):
             pick(high[i][:, 0, :], 2, *nodes(i), False)
 
         y0 = weight_tiles("y0", ((Y, 0),), "y0")
         y1 = weight_tiles("y1", ((Y, 1),), "y1")
-        pick(woven[0][:, :, 3], 3, *nodes(0), True)
+        pick(high[0][:, 1, :], 3, *nodes(0), True)
         for i in range(1, PIECES - 1):
             pick(high[i][:, 1, :], 3, *nodes(i), False)
         pick(high[3][:, 1, P:], 3, S - P, S, False)
@@ -185,6 +185,7 @@ def tile_picked_edgeatt_sigmoid_e_kernel(tc, xT, w1, w2, w3, offs, src, dst, out
         nc.scalar.copy(out=woven[3][:, 64:P, 2:], in_=high[3][:, :, 64:P].rearrange("p e n -> p n e"))
         regroup(y0[0], w1_first[:], True)
         regroup(y1[0], w1_second[:], False)
+        weave(0, 2, high[0][:])
         weave(1, 2, high[1][:])
         quantise_x(0)
         quantise_w(*y0)

@@ -176,23 +176,24 @@ def tile_picked_edgeatt_sigmoid_e_kernel(tc, xT, w1, w2, w3, offs, src, dst, out
 
         y0 = weight_tiles("y0", ((Y, 0),), "y0")
         y1 = weight_tiles("y1", ((Y, 1),), "y1")
-        pick(high[0][:, 1, :], 3, *nodes(0), True)
+        pick(high[0][:, 1, :P], 3, 0, P, True)
+        pick(high[0][:, 1, P:], 3, P, PIECE, True)
         for i in range(1, PIECES - 1):
             pick(high[i][:, 1, :], 3, *nodes(i), False)
         pick(high[3][:, 1, P:], 3, S - P, S, False)
         pick(high[3][:, 1, :P], 3, S - PIECE, S - P, False)
         nc.scalar.copy(out=woven[3][:, P:, 2:], in_=high[3][:, :, P:].rearrange("p e n -> p n e"))
-        nc.scalar.copy(out=woven[3][:, 64:P, 2:], in_=high[3][:, :, 64:P].rearrange("p e n -> p n e"))
+        nc.scalar.copy(out=woven[3][:, :P, 2:], in_=high[3][:, :, :P].rearrange("p e n -> p n e"))
         regroup(y0[0], w1_first[:], True)
         regroup(y1[0], w1_second[:], False)
-        weave(0, 2, high[0][:])
+        for lo in (0, P):
+            nc.vector.tensor_copy(out=woven[0][:, lo : lo + P, 2:], in_=high[0][:, :, lo : lo + P].rearrange("p e n -> p n e"))
         weave(1, 2, high[1][:])
         quantise_x(0)
         quantise_w(*y0)
         weave(2, 2, high[2][:])
         quantise_x(1)
         quantise_x(2)
-        nc.vector.tensor_copy(out=woven[3][:, :64, 2:], in_=high[3][:, :, :64].rearrange("p e n -> p n e"))
         quantise_x(3, P, PIECE)
         quantise_x(3, 0, P)
         quantise_w(*y1)

@@ -165,9 +165,10 @@ def tile_picked_edgeatt_sigmoid_e_kernel(tc, xT, w1, w2, w3, offs, src, dst, out
         def store(b, lo, hi):
             nc.sync.dma_start(out=out[b * P : (b + 1) * P, lo:hi], in_=result[b][:, lo:hi])
 
-        for j in range(2):
-            pick(low[:, j, :BANK], j, 0, BANK, True)
-            pick(low[:, j, BANK:], j, BANK, S, False)
+        pick(low[:, 0, :BANK], 0, 0, BANK, True)
+        pick(low[:, 0, BANK:], 0, BANK, S, False)
+        for i in range(PIECES):
+            pick(low[:, 1, i * PIECE : (i + 1) * PIECE], 1, *nodes(i), i == 0)
         for i in range(PIECES):
             weave(i, 0, low[:, :, i * PIECE : (i + 1) * PIECE])
         pick(high[0][:, 0, :], 2, *nodes(0), True)

@@ -22,20 +22,15 @@ BANK = 512
 STRIPE = 16
 Y, E, H = 0, 1, 2
 HALVES = ((0, BANK), (BANK, 2 * BANK))
-
 PIECE = 256
 PIECES = S // PIECE
-
+ROW_ORDER = (2, 0, 1, 3)
 FUSED = 512
 FETCHED = ((FUSED, 832), (832, U))
 
 
 def entries(offsets, lo, hi):
     return offsets[:, lo // STRIPE : hi // STRIPE]
-
-
-def nodes(i):
-    return i * PIECE, (i + 1) * PIECE
 
 
 def tile_picked_edgeatt_sigmoid_e_kernel(tc, xT, w1, w2, w3, offs, src, dst, out):
@@ -49,11 +44,11 @@ def tile_picked_edgeatt_sigmoid_e_kernel(tc, xT, w1, w2, w3, offs, src, dst, out
         src_sb = keep.tile([P, U // STRIPE], U16, name="src_sb")
         dst_sb = keep.tile([P, U // STRIPE], U16, name="dst_sb")
 
-        row = []
-        for j in range(PACK):
-            row.append(keep.tile([P, T], F32, name="row%d" % j))
+        row = {}
+        for j in ROW_ORDER:
+            row[j] = keep.tile([P, T], F32, name="row%d" % j)
             nc.sync.dma_start(out=row[j][:], in_=x_rows[:, j, :])
-            if j == 0:
+            if j == ROW_ORDER[0]:
                 nc.sync.dma_start(offs_sb[:], offs)
 
         def load_w(name, w, lo, hi):
@@ -68,9 +63,9 @@ def tile_picked_edgeatt_sigmoid_e_kernel(tc, xT, w1, w2, w3, offs, src, dst, out
         nc.sync.dma_start(dst_sb[:], dst)
         nc.sync.dma_start(src_sb[:], src)
 
-        low = keep.tile([P, 2, S], BF16, name="low", align_bytes=64)
-        high = {i: keep.tile([P, 2, PIECE], BF16, name="high%d" % i, align_bytes=64) for i in range(PIECES)}
         woven = [keep.tile([P, PIECE, PACK], BF16, name="woven%d" % i, tag="woven%d" % i, align_bytes=64) for i in range(PIECES)]
+        low = keep.tile([P, 2, S - PIECE], BF16, name="low", align_bytes=64)
+        high = keep.tile([P, 2, PIECE], BF16, name="high", align_bytes=64)
 
         def gather(target, window, on_vector):
             if on_vector:
@@ -81,8 +76,11 @@ def tile_picked_edgeatt_sigmoid_e_kernel(tc, xT, w1, w2, w3, offs, src, dst, out
         def pick(target, j, lo, hi, on_vector):
             gather(target, row[j][:].indirect(entries(offs_sb, lo, hi)), on_vector)
 
-        def weave(i, first, two_rows):
-            nc.vector.tensor_copy(out=woven[i][:, :, first : first + 2], in_=two_rows.rearrange("p e n -> p n e"))
+        def place(j, i, lo=0, hi=PIECE):
+            pick(woven[i][:, lo:hi, j], j, i * PIECE + lo, i * PIECE + hi, False)
+
+        def weave(target, two_rows):
+            nc.vector.tensor_copy(out=target, in_=two_rows.rearrange("p e n -> p n e"))
 
         w_codes, w_scales = {}, {}
 
@@ -165,39 +163,37 @@ def tile_picked_edgeatt_sigmoid_e_kernel(tc, xT, w1, w2, w3, offs, src, dst, out
         def store(b, lo, hi):
             nc.sync.dma_start(out=out[b * P : (b + 1) * P, lo:hi], in_=result[b][:, lo:hi])
 
-        pick(low[:, 0, :BANK], 0, 0, BANK, True)
-        pick(low[:, 0, BANK:], 0, BANK, S, False)
-        for i in range(PIECES):
-            pick(low[:, 1, i * PIECE : (i + 1) * PIECE], 1, *nodes(i), i == 0)
-        for i in range(PIECES):
-            weave(i, 0, low[:, :, i * PIECE : (i + 1) * PIECE])
-        pick(high[0][:, 0, :], 2, *nodes(0), True)
+        pick(high[:, 0, :], 2, 0, PIECE, True)
         for i in range(1, PIECES):
-            pick(high[i][:, 0, :], 2, *nodes(i), False)
+            place(2, i)
+        pick(low[:, 0, :], 0, 0, S - PIECE, True)
+        place(0, PIECES - 1)
+        pick(low[:, 1, :PIECE], 1, 0, PIECE, True)
+        for i in (1, 2):
+            pick(low[:, 1, i * PIECE : (i + 1) * PIECE], 1, i * PIECE, (i + 1) * PIECE, False)
+        place(1, PIECES - 1)
+        for i in (1, 0, 2):
+            weave(woven[i][:, :, :2], low[:, :, i * PIECE : (i + 1) * PIECE])
 
         y0 = weight_tiles("y0", ((Y, 0),), "y0")
         y1 = weight_tiles("y1", ((Y, 1),), "y1")
-        pick(high[0][:, 1, :P], 3, 0, P, True)
-        pick(high[0][:, 1, P:], 3, P, PIECE, True)
-        for i in range(1, PIECES - 1):
-            pick(high[i][:, 1, :], 3, *nodes(i), False)
-        pick(high[3][:, 1, P:], 3, S - P, S, False)
-        pick(high[3][:, 1, :P], 3, S - PIECE, S - P, False)
-        nc.scalar.copy(out=woven[3][:, P:, 2:], in_=high[3][:, :, P:].rearrange("p e n -> p n e"))
-        nc.scalar.copy(out=woven[3][:, :P, 2:], in_=high[3][:, :, :P].rearrange("p e n -> p n e"))
-        regroup(y0[0], w1_first[:], True)
-        regroup(y1[0], w1_second[:], False)
         for lo in (0, P):
-            nc.vector.tensor_copy(out=woven[0][:, lo : lo + P, 2:], in_=high[0][:, :, lo : lo + P].rearrange("p e n -> p n e"))
-        weave(1, 2, high[1][:])
+            pick(high[:, 1, lo : lo + P], 3, lo, lo + P, True)
+        place(3, 1)
+        place(3, 2)
+        place(3, 3, 0, P)
+        place(3, 3, P, PIECE)
+        for lo in (0, P):
+            weave(woven[0][:, lo : lo + P, 2:], high[:, :, lo : lo + P])
+        regroup(y0[0], w1_first[:], True)
         quantise_x(0)
         quantise_w(*y0)
-        weave(2, 2, high[2][:])
         quantise_x(1)
+        regroup(y1[0], w1_second[:], True)
         quantise_x(2)
-        quantise_x(3, P, PIECE)
-        quantise_x(3, 0, P)
         quantise_w(*y1)
+        quantise_x(3, 0, P)
+        quantise_x(3, P, PIECE)
         e0 = weight_tiles("e0", ((E, 0),), "woven2")
         e1 = weight_tiles("e1", ((E, 1),), "woven3")
         regroup(e0[0], w2_raw[:, :, :P], True)
@@ -207,11 +203,11 @@ def tile_picked_edgeatt_sigmoid_e_kernel(tc, xT, w1, w2, w3, offs, src, dst, out
         h = weight_tiles("h", ((H, 0), (H, 1)), "woven3")
         nc.gpsimd.tensor_scalar(h[0][:], w3_raw[:].rearrange("p j n -> p n j"), 1.0, 0.0, MULT, ADD)
 
-        res[Y, 0] = keep.tile([P, S], F32, name="res_y0", tag="w1_second")
+        res[Y, 0] = keep.tile([P, S], F32, name="res_y0")
         for i in range(PIECES - 1):
-            product(Y, 0, *nodes(i), i)
-        product(Y, 0, S - P, S, 3)
-        product(Y, 0, S - PIECE, S - P, 4)
+            product(Y, 0, i * PIECE, (i + 1) * PIECE, i)
+        product(Y, 0, S - PIECE, S - P, 3)
+        product(Y, 0, S - P, S, 4)
         for half in HALVES:
             fetch_y(0, *half, True)
         quantise_w(*h)

@@ -64,7 +64,7 @@ def tile_picked_edgeatt_sigmoid_e_kernel(tc, xT, w1, w2, w3, offs, src, dst, out
         nc.sync.dma_start(src_sb[:], src)
 
         woven = [keep.tile([P, PIECE, PACK], BF16, name="woven%d" % i, tag="woven%d" % i, align_bytes=64) for i in range(PIECES)]
-        low = keep.tile([P, 2, S - PIECE], BF16, name="low", align_bytes=64)
+        low = keep.tile([P, 2, BANK], BF16, name="low", align_bytes=64)
         high = keep.tile([P, 2, PIECE], BF16, name="high", align_bytes=64)
 
         def gather(target, window, on_vector):
@@ -166,17 +166,18 @@ def tile_picked_edgeatt_sigmoid_e_kernel(tc, xT, w1, w2, w3, offs, src, dst, out
         pick(high[:, 0, :], 2, 0, PIECE, True)
         for i in range(1, PIECES):
             place(2, i)
-        pick(low[:, 0, :], 0, 0, S - PIECE, True)
-        place(0, PIECES - 1)
-        pick(low[:, 1, :PIECE], 1, 0, PIECE, True)
-        for i in (1, 2):
-            pick(low[:, 1, i * PIECE : (i + 1) * PIECE], 1, i * PIECE, (i + 1) * PIECE, False)
-        place(1, PIECES - 1)
-        for i in (1, 0, 2):
+        pick(low[:, 0, :], 0, 0, BANK, True)
+        place(0, 2)
+        place(0, 3)
+        pick(low[:, 1, PIECE:], 1, PIECE, BANK, True)
+        pick(low[:, 1, :P], 1, 0, P, False)
+        pick(low[:, 1, P:PIECE], 1, P, PIECE, True)
+        place(1, 2)
+        place(1, 3)
+        for i in (1, 0):
             weave(woven[i][:, :, :2], low[:, :, i * PIECE : (i + 1) * PIECE])
 
         y0 = weight_tiles("y0", ((Y, 0),), "y0")
-        y1 = weight_tiles("y1", ((Y, 1),), "y1")
         for lo in (0, P):
             pick(high[:, 1, lo : lo + P], 3, lo, lo + P, True)
         place(3, 1)
@@ -189,11 +190,12 @@ def tile_picked_edgeatt_sigmoid_e_kernel(tc, xT, w1, w2, w3, offs, src, dst, out
         quantise_x(0)
         quantise_w(*y0)
         quantise_x(1)
+        y1 = weight_tiles("y1", ((Y, 1),), "y1")
         regroup(y1[0], w1_second[:], True)
         quantise_x(2)
-        quantise_w(*y1)
         quantise_x(3, 0, P)
         quantise_x(3, P, PIECE)
+        quantise_w(*y1)
         e0 = weight_tiles("e0", ((E, 0),), "woven2")
         e1 = weight_tiles("e1", ((E, 1),), "woven3")
         regroup(e0[0], w2_raw[:, :, :P], True)

@@ -25,8 +25,10 @@ HALVES = ((0, BANK), (BANK, 2 * BANK))
 PIECE = 256
 PIECES = S // PIECE
 ROW_ORDER = (2, 0, 1, 3)
-FUSED = 512
-FETCHED = ((FUSED, 832), (832, U))
+FIRST_GATE = 384
+LAST_GATE = 320
+FUSED = 576
+FETCHED = ((FUSED, 864), (864, U))
 
 
 def entries(offsets, lo, hi):
@@ -227,17 +229,17 @@ def tile_picked_edgeatt_sigmoid_e_kernel(tc, xT, w1, w2, w3, offs, src, dst, out
         product(H, 0, *HALVES[1], 4)
         for half in HALVES:
             add_e(1, *half)
-        for half in HALVES:
-            squash(0, *half)
-            times_h(0, *half)
+        for part in ((0, FIRST_GATE), (FIRST_GATE, U)):
+            squash(0, *part)
+            times_h(0, *part)
         store(0, 0, U)
         product(H, 1, *HALVES[0], 5)
         product(H, 1, *HALVES[1], 6)
-        squash(1, 0, FUSED)
-        squash(1, FUSED, U)
+        squash(1, 0, LAST_GATE)
+        squash(1, LAST_GATE, U)
         for lo, hi in FETCHED:
             gather(h_src[:, lo - FUSED : hi - FUSED], res[H, 1][:].indirect(entries(src_sb, lo, hi)), False)
-        for part in ((0, FUSED // 2), (FUSED // 2, FUSED)):
+        for part in ((0, LAST_GATE), (LAST_GATE, FUSED)):
             times_h(1, *part)
             store(1, *part)
         for lo, hi in FETCHED:

from contextlib import ExitStack

import concourse.mybir as mybir

K, T, S, N, U = 512, 2048, 1024, 256, 1024
FLOPS = 3 * 2 * K * N * S

F32 = mybir.dt.float32
BF16 = mybir.dt.bfloat16
U32 = mybir.dt.uint32
U16 = mybir.dt.uint16
U8 = mybir.dt.uint8
FP8X4 = mybir.dt.float8_e4m3fn_x4
ADD = mybir.AluOpType.add
MULT = mybir.AluOpType.mult
SIGMOID = mybir.ActivationFunctionType.Sigmoid
COPY = mybir.ActivationFunctionType.Copy

P = 128
PACK = 4
BANK = 512
STRIPE = 16
Y, E, H = 0, 1, 2
HALVES = ((0, BANK), (BANK, 2 * BANK))
PIECE = 256
PIECES = S // PIECE
ROW_ORDER = (2, 0, 1, 3)
FIRST_GATE = 384
LAST_GATE = 320
FUSED = 576
FETCHED = ((FUSED, 864), (864, U))


def entries(offsets, lo, hi):
    return offsets[:, lo // STRIPE : hi // STRIPE]


def tile_picked_edgeatt_sigmoid_e_kernel(tc, xT, w1, w2, w3, offs, src, dst, out):
    nc = tc.nc
    with ExitStack() as ctx:
        keep = ctx.enter_context(tc.tile_pool(name="keep", bufs=1))
        psum = ctx.enter_context(tc.psum_pool(name="psum", bufs=1))

        x_rows = xT.rearrange("(p j) t -> p j t", j=PACK)
        offs_sb = keep.tile([P, S // STRIPE], U16, name="offs_sb")
        src_sb = keep.tile([P, U // STRIPE], U16, name="src_sb")
        dst_sb = keep.tile([P, U // STRIPE], U16, name="dst_sb")

        row = {}
        for j in ROW_ORDER:
            row[j] = keep.tile([P, T], F32, name="row%d" % j)
            nc.sync.dma_start(out=row[j][:], in_=x_rows[:, j, :])
            if j == ROW_ORDER[0]:
                nc.sync.dma_start(offs_sb[:], offs)

        def load_w(name, w, lo, hi):
            tile = keep.tile([P, PACK, hi - lo], F32, name=name)
            nc.sync.dma_start(out=tile[:], in_=w.rearrange("(p j) n -> p j n", j=PACK)[:, :, lo:hi])
            return tile

        w1_first = load_w("w1_first", w1, 0, P)
        w1_second = load_w("w1_second", w1, P, N)
        w2_raw = load_w("w2_raw", w2, 0, N)
        w3_raw = load_w("w3_raw", w3, 0, N)
        nc.sync.dma_start(dst_sb[:], dst)
        nc.sync.dma_start(src_sb[:], src)

        woven = [keep.tile([P, PIECE, PACK], BF16, name="woven%d" % i, tag="woven%d" % i, align_bytes=64) for i in range(PIECES)]
        low = keep.tile([P, 2, BANK], BF16, name="low", align_bytes=64)
        high = keep.tile([P, 2, PIECE], BF16, name="high", align_bytes=64)

        def gather(target, window, on_vector):
            if on_vector:
                nc.vector.tensor_copy(out=target, in_=window)
            else:
                nc.scalar.activation(target, window, COPY)

        def pick(target, j, lo, hi, on_vector):
            gather(target, row[j][:].indirect(entries(offs_sb, lo, hi)), on_vector)

        def place(j, i, lo=0, hi=PIECE):
            pick(woven[i][:, lo:hi, j], j, i * PIECE + lo, i * PIECE + hi, False)

        def weave(target, two_rows):
            nc.vector.tensor_copy(out=target, in_=two_rows.rearrange("p e n -> p n e"))

        w_codes, w_scales = {}, {}

        def weight_tiles(name, members, tag):
            grouped = keep.tile([P, len(members) * P, PACK], BF16, name="w_grouped_" + name, tag=tag, align_bytes=64)
            codes = keep.tile([P, len(members) * P], U32, name="w_codes_" + name, align_bytes=64)
            scales = keep.tile([P, len(members) * P], U8, name="w_scales_" + name, align_bytes=64)
            for place, member in enumerate(members):
                cols = slice(place * P, (place + 1) * P)
                w_codes[member], w_scales[member] = codes[:, cols], scales[:, cols]
            return grouped, codes, scales

        def regroup(grouped, raw, on_vector):
            target = grouped[:].rearrange("p (c i) j -> p c j i", i=4)
            source = raw.rearrange("p j (c i) -> p c j i", i=4)
            if on_vector:
                nc.vector.tensor_copy(out=target, in_=source)
            else:
                nc.scalar.copy(out=target, in_=source)

        def quantise_w(grouped, codes, scales):
            nc.vector.quantize_mx(out=codes[:].bitcast(FP8X4), scales=scales[:], in_=grouped[:].rearrange("p n j -> p (n j)"))

        x_codes = [keep.tile([P, BANK], U32, name="x_codes%d" % half, align_bytes=64) for half in range(2)]
        x_scales = [keep.tile([P, BANK], U8, name="x_scales%d" % half, align_bytes=64) for half in range(2)]

        def quantise_x(i, lo=0, hi=PIECE):
            half, first = divmod(i * PIECE, BANK)
            nc.vector.quantize_mx(
                out=x_codes[half][:, first + lo : first + hi].bitcast(FP8X4),
                scales=x_scales[half][:, first + lo : first + hi],
                in_=woven[i][:, lo:hi, :].rearrange("p n j -> p (n j)"),
            )

        res = {}
        for m, b in ((E, 0), (E, 1), (H, 0), (H, 1)):
            spare = STRIPE if (m, b) == (E, 0) else 0
            res[m, b] = keep.tile([P, S + spare], F32, name="res%d_%d" % (m, b))
        nc.gpsimd.memset(res[E, 0][:, S:], 0.0)

        warm = keep.tile([P, 1], F32, name="warm")
        nc.scalar.activation(warm[:], res[E, 0][:, S : S + 1], SIGMOID)

        def product(m, b, lo, hi, bank, on_vector=False):
            acc = psum.tile([P, BANK], F32, name="acc", tag="bank%d" % bank)
            half, first = divmod(lo, BANK)
            cols = slice(first, first + hi - lo)
            nc.tensor.matmul_mx(
                out=acc[:, : hi - lo],
                lhsT=w_codes[m, b].bitcast(FP8X4),
                lhsT_scale=w_scales[m, b],
                rhs=x_codes[half][:, cols].bitcast(FP8X4),
                rhs_scale=x_scales[half][:, cols],
                start=True,
                stop=True,
            )
            if on_vector:
                nc.vector.tensor_copy(out=res[m, b][:, lo:hi], in_=acc[:, : hi - lo])
            else:
                nc.scalar.copy(out=res[m, b][:, lo:hi], in_=acc[:, : hi - lo])

        y_dst = [keep.tile([P, U], F32, name="y_dst%d" % b) for b in range(2)]
        logit = [keep.tile([P, U], F32, name="logit%d" % b) for b in range(2)]
        gate = [keep.tile([P, U], F32, name="gate%d" % b) for b in range(2)]
        result = [keep.tile([P, U], F32, name="result%d" % b) for b in range(2)]
        h_src = keep.tile([P, U - FUSED], F32, name="h_src")

        def fetch_y(b, lo, hi, on_vector):
            gather(y_dst[b][:, lo:hi], res[Y, b][:].indirect(entries(dst_sb, lo, hi)), on_vector)

        def add_e(b, lo, hi):
            nc.vector.tensor_tensor(logit[b][:, lo:hi], res[E, b][:].indirect(entries(src_sb, lo, hi)), y_dst[b][:, lo:hi], ADD)

        def squash(b, lo, hi):
            nc.scalar.activation(gate[b][:, lo:hi], logit[b][:, lo:hi], SIGMOID)

        def times_h(b, lo, hi):
            nc.vector.tensor_tensor(result[b][:, lo:hi], res[H, b][:].indirect(entries(src_sb, lo, hi)), gate[b][:, lo:hi], MULT)

        def store(b, lo, hi):
            nc.sync.dma_start(out=out[b * P : (b + 1) * P, lo:hi], in_=result[b][:, lo:hi])

        pick(high[:, 0, :], 2, 0, PIECE, True)
        for i in range(1, PIECES):
            place(2, i)
        pick(low[:, 0, :], 0, 0, BANK, True)
        place(0, 2)
        place(0, 3)
        pick(low[:, 1, PIECE:], 1, PIECE, BANK, True)
        pick(low[:, 1, :P], 1, 0, P, False)
        pick(low[:, 1, P:PIECE], 1, P, PIECE, True)
        place(1, 2)
        place(1, 3)
        for i in (1, 0):
            weave(woven[i][:, :, :2], low[:, :, i * PIECE : (i + 1) * PIECE])

        y0 = weight_tiles("y0", ((Y, 0),), "y0")
        for lo in (0, P):
            pick(high[:, 1, lo : lo + P], 3, lo, lo + P, True)
        place(3, 1)
        place(3, 2)
        place(3, 3, 0, P)
        place(3, 3, P, PIECE)
        for lo in (0, P):
            weave(woven[0][:, lo : lo + P, 2:], high[:, :, lo : lo + P])
        regroup(y0[0], w1_first[:], True)
        quantise_x(0)
        quantise_w(*y0)
        quantise_x(1)
        y1 = weight_tiles("y1", ((Y, 1),), "y1")
        regroup(y1[0], w1_second[:], True)
        quantise_x(2)
        quantise_x(3, 0, P)
        quantise_x(3, P, PIECE)
        quantise_w(*y1)
        e0 = weight_tiles("e0", ((E, 0),), "woven2")
        e1 = weight_tiles("e1", ((E, 1),), "woven3")
        regroup(e0[0], w2_raw[:, :, :P], True)
        regroup(e1[0], w2_raw[:, :, P:], True)
        quantise_w(*e0)
        quantise_w(*e1)
        h = weight_tiles("h", ((H, 0), (H, 1)), "woven3")
        nc.gpsimd.tensor_scalar(h[0][:], w3_raw[:].rearrange("p j n -> p n j"), 1.0, 0.0, MULT, ADD)

        res[Y, 0] = keep.tile([P, S], F32, name="res_y0")
        for i in range(PIECES - 1):
            product(Y, 0, i * PIECE, (i + 1) * PIECE, i)
        product(Y, 0, S - PIECE, S - P, 3)
        product(Y, 0, S - P, S, 4)
        for half in HALVES:
            fetch_y(0, *half, True)
        quantise_w(*h)
        res[Y, 1] = keep.tile([P, S], F32, name="res_y1", tag="w_codes_y0", align_bytes=64)
        product(Y, 1, *HALVES[0], 5)
        product(Y, 1, *HALVES[1], 6)
        product(E, 0, *HALVES[0], 7)
        product(E, 0, *HALVES[1], 0)
        product(E, 1, *HALVES[0], 1)
        fetch_y(1, *HALVES[0], False)
        product(E, 1, *HALVES[1], 2)
        add_e(0, 0, U)
        fetch_y(1, *HALVES[1], False)
        product(H, 0, *HALVES[0], 3)
        product(H, 0, *HALVES[1], 4)
        for half in HALVES:
            add_e(1, *half)
        for part in ((0, FIRST_GATE), (FIRST_GATE, U)):
            squash(0, *part)
            times_h(0, *part)
        store(0, 0, U)
        product(H, 1, *HALVES[0], 5)
        product(H, 1, *HALVES[1], 6)
        squash(1, 0, LAST_GATE)
        squash(1, LAST_GATE, U)
        for lo, hi in FETCHED:
            gather(h_src[:, lo - FUSED : hi - FUSED], res[H, 1][:].indirect(entries(src_sb, lo, hi)), False)
        for part in ((0, LAST_GATE), (LAST_GATE, FUSED)):
            times_h(1, *part)
            store(1, *part)
        for lo, hi in FETCHED:
            nc.vector.tensor_tensor(result[1][:, lo:hi], h_src[:, lo - FUSED : hi - FUSED], gate[1][:, lo:hi], MULT)
            store(1, lo, hi)
